import numpy as np
import ml_dtypes


def mxq(x, axis, fmt="e4m3"):
    dtype, down = {"e4m3": (ml_dtypes.float8_e4m3fn, 7), "e5m2": (ml_dtypes.float8_e5m2, 14)}[fmt]
    v = np.moveaxis(np.asarray(x, np.float32).astype(ml_dtypes.bfloat16).astype(np.float64), axis, -1)
    blocks = v.reshape(v.shape[:-1] + (-1, 32))
    amax = np.abs(blocks).max(-1, keepdims=True)
    byte = np.maximum(np.where(amax > 0, np.frexp(amax)[1] - 1 + 127, 0) - down, 1)
    scale = np.exp2(byte - 127.0)
    codes = (blocks / scale).astype(np.float32).astype(dtype).astype(np.float64)
    return np.moveaxis((codes * scale).reshape(v.shape), -1, axis)


WIDE = False


def mx_kscale(k):
    if not WIDE:
        return np.ones(k)
    levels = np.array([10, -10, 5, -5, 0])
    if k % 512:
        return np.exp2(np.random.permutation(np.resize(levels, k // 32))).repeat(32)
    a = np.empty((k // 512, 16))
    for p in range(k // 512):
        a[p, :8] = np.random.permutation(np.resize(levels, 8))
        for g in range(8):
            far = levels[np.abs(levels - a[p, g]) >= 10]
            a[p, g + 8] = far[np.random.randint(len(far))]
    return np.exp2(a.ravel()).repeat(32)


def f64(x):
    return np.asarray(x).astype(np.float64)


def striped(idx):
    return np.tile(idx.reshape(-1, 16).T, (8, 1)).astype(np.uint16)


def unstriped(offs):
    return offs[:16].T.reshape(-1).astype(np.int64)


K, T, S, N, U = 512, 1024, 512, 256, 1024


def setup_inputs():
    n = np.random.standard_normal
    s = mx_kscale(K)[:, None]
    return {
        "xT": (n((K, T)) * s).astype(np.float32),
        "mem": n((N, U)).astype(np.float32),
        "w1": (n((K, N)) / np.sqrt(K) / s).astype(np.float32),
        "offs": striped(np.random.permutation(T)[:S]),
        "slot": striped(np.random.permutation(U)[:S]),
    }


def reference(xT, mem, w1, offs, slot):
    xq = mxq(f64(xT)[:, unstriped(offs)], 0, "e4m3")
    y = mxq(f64(w1), 0, "e4m3").T @ xq
    out = f64(mem).copy()
    out[:, unstriped(slot)] = np.minimum(f64(mem)[:, unstriped(slot)], y)
    return out

@@ -1,0 +1,113 @@
+from contextlib import ExitStack
+
+import concourse.mybir as mybir
+
+K, T, S, N, U = 512, 1024, 512, 256, 1024
+FLOPS = 2 * K * S * N
+
+F32 = mybir.dt.float32
+BF16 = mybir.dt.bfloat16
+U32 = mybir.dt.uint32
+U16 = mybir.dt.uint16
+U8 = mybir.dt.uint8
+FP8X4 = mybir.dt.float8_e4m3fn_x4
+COPY = mybir.ActivationFunctionType.Copy
+MIN = mybir.AluOpType.min
+
+P = 128
+PACK = 4
+HALF = S // 2
+LIST_ROWS = 16
+VECTOR_CASTS = 2
+
+
+def quantize(nc, pool, grouped, width, name, tag=None):
+    codes = pool.tile([P, width], U32, name=name + "_codes", tag=tag or name + "_codes", align_bytes=64)
+    scales = pool.tile([P, width], U8, name=name + "_scales", align_bytes=64)
+    nc.vector.quantize_mx(out=codes[:].bitcast(FP8X4), scales=scales[:], in_=grouped[:].rearrange("p c j -> p (c j)"))
+    return codes, scales
+
+
+def tile_picked_idxput_min_e_kernel(tc, xT, mem, w1, offs, slot, out):
+    nc = tc.nc
+    with ExitStack() as ctx:
+        sb = ctx.enter_context(tc.tile_pool(name="sb", bufs=1))
+        psum = ctx.enter_context(tc.psum_pool(name="psum", bufs=1))
+
+        offs_sb = sb.tile([P, S // LIST_ROWS], U16, name="offs_sb")
+        slot_sb = sb.tile([P, S // LIST_ROWS], U16, name="slot_sb")
+        x_rows = [sb.tile([P, T], F32, name=f"x_rows{j}") for j in range(PACK)]
+        w_rows = sb.tile([P, PACK, N], F32, name="w_rows")
+        store = [sb.tile([P, U], F32, name=f"store{b}") for b in range(N // P)]
+
+        x_by_row = xT.rearrange("(p j) t -> p j t", j=PACK)
+        nc.sync.dma_start(x_rows[0][:], x_by_row[:, 0, :])
+        nc.sync.dma_start(offs_sb[:], offs)
+        for j in range(1, PACK - 1):
+            nc.sync.dma_start(x_rows[j][:], x_by_row[:, j, :])
+        nc.sync.dma_start(w_rows[:], w1.rearrange("(p j) m -> p j m", j=PACK))
+        nc.sync.dma_start(x_rows[PACK - 1][:], x_by_row[:, PACK - 1, :])
+        nc.sync.dma_start(slot_sb[:], slot)
+        for b in range(N // P):
+            nc.sync.dma_start(store[b][:], mem[b * P : (b + 1) * P, :])
+
+        warm = sb.tile([P, 8], F32, name="warm")
+        warm2 = sb.tile([P, 8], F32, name="warm2")
+        nc.vector.memset(warm[:], 0.0)
+        nc.scalar.activation(warm2[:], warm[:], COPY)
+
+        offs_half = [offs_sb[:, h * HALF // LIST_ROWS : (h + 1) * HALF // LIST_ROWS] for h in range(2)]
+        slot_half = [slot_sb[:, h * HALF // LIST_ROWS : (h + 1) * HALF // LIST_ROWS] for h in range(2)]
+
+        picked = [sb.tile([P, HALF, PACK], BF16, name=f"picked{h}", align_bytes=64) for h in range(2)]
+        for j in range(PACK):
+            x_bf = sb.tile([P, T], BF16, name=f"x_bf{j}")
+            if j == 1:
+                nc.vector.tensor_copy(x_bf[:], x_rows[j][:])
+            else:
+                nc.scalar.copy(x_bf[:], x_rows[j][:])
+            nc.vector.tensor_copy(picked[0][:, :, j], x_rows[j][:].indirect(offs_half[0]))
+            nc.scalar.activation(picked[1][:, :, j], x_bf[:].indirect(offs_half[1]), COPY)
+
+        w_grouped = sb.tile([P, N, PACK], BF16, name="w_grouped", align_bytes=64)
+        nc.vector.tensor_copy(
+            w_grouped[:].rearrange("p (c i) j -> p c j i", i=4),
+            w_rows[:].rearrange("p j (c i) -> p c j i", i=4),
+        )
+        wq = quantize(nc, sb, w_grouped, N, "wq")
+
+        def product(y, b, xq):
+            nc.tensor.matmul_mx(
+                out=y,
+                lhsT=wq[0][:, b * P : (b + 1) * P].bitcast(FP8X4),
+                lhsT_scale=wq[1][:, b * P : (b + 1) * P],
+                rhs=xq[0][:].bitcast(FP8X4),
+                rhs_scale=xq[1][:],
+                start=True,
+                stop=True,
+            )
+
+        y0 = [psum.tile([P, HALF], F32, name=f"y0{h}") for h in range(2)]
+        y1 = psum.tile([P, S], F32, name="y1")
+        old0 = [sb.tile([P, HALF], F32, name=f"old0{h}", align_bytes=64) for h in range(2)]
+        new0 = [sb.tile([P, HALF], F32, name=f"new0{h}") for h in range(2)]
+        old1 = sb.tile([P, S], F32, name="old1")
+        new1 = sb.tile([P, S], F32, name="new1")
+
+        xq0 = quantize(nc, sb, picked[0], HALF, "xq0")
+        product(y0[0][:], 0, xq0)
+        product(y1[:, 0:HALF], 1, xq0)
+        for h in range(2):
+            nc.vector.tensor_copy(old0[h][:], store[0][:].indirect(slot_half[h]))
+        nc.vector.tensor_tensor(new0[0][:], y0[0][:], old0[0][:], MIN)
+        nc.vector.tensor_copy(store[0][:].indirect(slot_half[0]), new0[0][:])
+        xq1 = quantize(nc, sb, picked[1], HALF, "xq1", tag="old00")
+        product(y0[1][:], 0, xq1)
+        product(y1[:, HALF:S], 1, xq1)
+        nc.vector.tensor_copy(old1[:], store[1][:].indirect(slot_sb[:]))
+        nc.vector.tensor_tensor(new0[1][:], y0[1][:], old0[1][:], MIN)
+        nc.vector.tensor_tensor(new1[:], y1[:], old1[:], MIN)
+        nc.vector.tensor_copy(store[0][:].indirect(slot_half[1]), new0[1][:])
+        nc.sync.dma_start(out[0:P, :], store[0][:])
+        nc.vector.tensor_copy(store[1][:].indirect(slot_sb[:]), new1[:])
+        nc.sync.dma_start(out[P : 2 * P, :], store[1][:])

@@ -43,18 +43,12 @@ def tile_picked_idxput_min_e_kernel(tc, xT, mem, w1, offs, slot, out):
         x_by_row = xT.rearrange("(p j) t -> p j t", j=PACK)
         nc.sync.dma_start(x_rows[0][:], x_by_row[:, 0, :])
         nc.sync.dma_start(offs_sb[:], offs)
-        for j in range(1, PACK - 1):
+        for j in range(1, PACK):
             nc.sync.dma_start(x_rows[j][:], x_by_row[:, j, :])
         nc.sync.dma_start(w_rows[:], w1.rearrange("(p j) m -> p j m", j=PACK))
-        nc.sync.dma_start(x_rows[PACK - 1][:], x_by_row[:, PACK - 1, :])
         nc.sync.dma_start(slot_sb[:], slot)
         for b in range(N // P):
             nc.sync.dma_start(store[b][:], mem[b * P : (b + 1) * P, :])
-
-        warm = sb.tile([P, 8], F32, name="warm")
-        warm2 = sb.tile([P, 8], F32, name="warm2")
-        nc.vector.memset(warm[:], 0.0)
-        nc.scalar.activation(warm2[:], warm[:], COPY)
 
         offs_half = [offs_sb[:, h * HALF // LIST_ROWS : (h + 1) * HALF // LIST_ROWS] for h in range(2)]
         slot_half = [slot_sb[:, h * HALF // LIST_ROWS : (h + 1) * HALF // LIST_ROWS] for h in range(2)]
@@ -69,18 +63,19 @@ def tile_picked_idxput_min_e_kernel(tc, xT, mem, w1, offs, slot, out):
             nc.vector.tensor_copy(picked[0][:, :, j], x_rows[j][:].indirect(offs_half[0]))
             nc.scalar.activation(picked[1][:, :, j], x_bf[:].indirect(offs_half[1]), COPY)
 
-        w_grouped = sb.tile([P, N, PACK], BF16, name="w_grouped", align_bytes=64)
-        nc.vector.tensor_copy(
-            w_grouped[:].rearrange("p (c i) j -> p c j i", i=4),
-            w_rows[:].rearrange("p j (c i) -> p c j i", i=4),
-        )
-        wq = quantize(nc, sb, w_grouped, N, "wq")
+        w_grouped = [sb.tile([P, P, PACK], BF16, name=f"w_grouped{b}", align_bytes=64) for b in range(N // P)]
+        for b in range(N // P):
+            nc.vector.tensor_copy(
+                w_grouped[b][:].rearrange("p (c i) j -> p c j i", i=4),
+                w_rows[:, :, b * P : (b + 1) * P].rearrange("p j (c i) -> p c j i", i=4),
+            )
+        wq = [quantize(nc, sb, w_grouped[b], P, f"wq{b}") for b in range(N // P)]
 
         def product(y, b, xq):
             nc.tensor.matmul_mx(
                 out=y,
-                lhsT=wq[0][:, b * P : (b + 1) * P].bitcast(FP8X4),
-                lhsT_scale=wq[1][:, b * P : (b + 1) * P],
+                lhsT=wq[b][0][:].bitcast(FP8X4),
+                lhsT_scale=wq[b][1][:],
                 rhs=xq[0][:].bitcast(FP8X4),
                 rhs_scale=xq[1][:],
                 start=True,

@@ -60,7 +60,10 @@ def tile_picked_idxput_min_e_kernel(tc, xT, mem, w1, offs, slot, out):
                 nc.vector.tensor_copy(x_bf[:], x_rows[j][:])
             else:
                 nc.scalar.copy(x_bf[:], x_rows[j][:])
-            nc.vector.tensor_copy(picked[0][:, :, j], x_rows[j][:].indirect(offs_half[0]))
+            piece = HALF if j < PACK - 1 else HALF // 2
+            for c in range(0, HALF, piece):
+                entries = offs_sb[:, c // LIST_ROWS : (c + piece) // LIST_ROWS]
+                nc.vector.tensor_copy(picked[0][:, c : c + piece, j], x_rows[j][:].indirect(entries))
             nc.scalar.activation(picked[1][:, :, j], x_bf[:].indirect(offs_half[1]), COPY)
 
         w_grouped = [sb.tile([P, P, PACK], BF16, name=f"w_grouped{b}", align_bytes=64) for b in range(N // P)]
@@ -89,7 +92,16 @@ def tile_picked_idxput_min_e_kernel(tc, xT, mem, w1, offs, slot, out):
         old1 = sb.tile([P, S], F32, name="old1")
         new1 = sb.tile([P, S], F32, name="new1")
 
-        xq0 = quantize(nc, sb, picked[0], HALF, "xq0")
+        xq0_codes = sb.tile([P, HALF], U32, name="xq0_codes", align_bytes=64)
+        xq0_scales = sb.tile([P, HALF], U8, name="xq0_scales", align_bytes=64)
+        for c in range(0, HALF, HALF // 2):
+            cols = slice(c, c + HALF // 2)
+            nc.vector.quantize_mx(
+                out=xq0_codes[:, cols].bitcast(FP8X4),
+                scales=xq0_scales[:, cols],
+                in_=picked[0][:, cols, :].rearrange("p c j -> p (c j)"),
+            )
+        xq0 = (xq0_codes, xq0_scales)
         product(y0[0][:], 0, xq0)
         product(y1[:, 0:HALF], 1, xq0)
         for h in range(2):

@@ -16,13 +16,15 @@ MIN = mybir.AluOpType.min
 
 P = 128
 PACK = 4
-HALF = S // 2
 LIST_ROWS = 16
-VECTOR_CASTS = 2
+BLOCKS = N // P
+VECTOR_ENTRIES = 160
+FIRST_CAST = 704
+VECTOR_W_COLUMNS = 80
 
 
-def quantize(nc, pool, grouped, width, name, tag=None):
-    codes = pool.tile([P, width], U32, name=name + "_codes", tag=tag or name + "_codes", align_bytes=64)
+def quantize(nc, pool, grouped, width, name):
+    codes = pool.tile([P, width], U32, name=name + "_codes", align_bytes=64)
     scales = pool.tile([P, width], U8, name=name + "_scales", align_bytes=64)
     nc.vector.quantize_mx(out=codes[:].bitcast(FP8X4), scales=scales[:], in_=grouped[:].rearrange("p c j -> p (c j)"))
     return codes, scales
@@ -38,83 +40,63 @@ def tile_picked_idxput_min_e_kernel(tc, xT, mem, w1, offs, slot, out):
         slot_sb = sb.tile([P, S // LIST_ROWS], U16, name="slot_sb")
         x_rows = [sb.tile([P, T], F32, name=f"x_rows{j}") for j in range(PACK)]
         w_rows = sb.tile([P, PACK, N], F32, name="w_rows")
-        store = [sb.tile([P, U], F32, name=f"store{b}") for b in range(N // P)]
+        store = [sb.tile([P, U], F32, name=f"store{b}") for b in range(BLOCKS)]
 
         x_by_row = xT.rearrange("(p j) t -> p j t", j=PACK)
         nc.sync.dma_start(x_rows[0][:], x_by_row[:, 0, :])
         nc.sync.dma_start(offs_sb[:], offs)
-        for j in range(1, PACK):
-            nc.sync.dma_start(x_rows[j][:], x_by_row[:, j, :])
-        nc.sync.dma_start(w_rows[:], w1.rearrange("(p j) m -> p j m", j=PACK))
         nc.sync.dma_start(slot_sb[:], slot)
-        for b in range(N // P):
-            nc.sync.dma_start(store[b][:], mem[b * P : (b + 1) * P, :])
+        nc.sync.dma_start(x_rows[1][:], x_by_row[:, 1, :])
+        nc.sync.dma_start(x_rows[2][:], x_by_row[:, 2, :])
+        nc.sync.dma_start(x_rows[3][:], x_by_row[:, 3, :])
+        nc.sync.dma_start(store[0][:], mem[0:P, :])
+        nc.sync.dma_start(w_rows[:], w1.rearrange("(p j) m -> p j m", j=PACK))
+        nc.sync.dma_start(store[1][:], mem[P : 2 * P, :])
 
-        offs_half = [offs_sb[:, h * HALF // LIST_ROWS : (h + 1) * HALF // LIST_ROWS] for h in range(2)]
-        slot_half = [slot_sb[:, h * HALF // LIST_ROWS : (h + 1) * HALF // LIST_ROWS] for h in range(2)]
-
-        picked = [sb.tile([P, HALF, PACK], BF16, name=f"picked{h}", align_bytes=64) for h in range(2)]
+        cut = VECTOR_ENTRIES // LIST_ROWS
+        picked = sb.tile([P, S, PACK], BF16, name="picked", align_bytes=64)
         for j in range(PACK):
             x_bf = sb.tile([P, T], BF16, name=f"x_bf{j}")
-            if j == 1:
-                nc.vector.tensor_copy(x_bf[:], x_rows[j][:])
+            if j == 0:
+                nc.vector.tensor_copy(x_bf[:, :FIRST_CAST], x_rows[j][:, :FIRST_CAST])
+                nc.scalar.copy(x_bf[:, FIRST_CAST:], x_rows[j][:, FIRST_CAST:])
             else:
-                nc.scalar.copy(x_bf[:], x_rows[j][:])
-            piece = HALF if j < PACK - 1 else HALF // 2
-            for c in range(0, HALF, piece):
-                entries = offs_sb[:, c // LIST_ROWS : (c + piece) // LIST_ROWS]
-                nc.vector.tensor_copy(picked[0][:, c : c + piece, j], x_rows[j][:].indirect(entries))
-            nc.scalar.activation(picked[1][:, :, j], x_bf[:].indirect(offs_half[1]), COPY)
+                nc.vector.tensor_copy(x_bf[:], x_rows[j][:])
+            nc.vector.tensor_copy(picked[:, :VECTOR_ENTRIES, j], x_rows[j][:].indirect(offs_sb[:, :cut]))
+            nc.scalar.activation(picked[:, VECTOR_ENTRIES:, j], x_bf[:].indirect(offs_sb[:, cut:]), COPY)
 
-        w_grouped = [sb.tile([P, P, PACK], BF16, name=f"w_grouped{b}", align_bytes=64) for b in range(N // P)]
-        for b in range(N // P):
-            nc.vector.tensor_copy(
-                w_grouped[b][:].rearrange("p (c i) j -> p c j i", i=4),
-                w_rows[:, :, b * P : (b + 1) * P].rearrange("p j (c i) -> p c j i", i=4),
-            )
-        wq = [quantize(nc, sb, w_grouped[b], P, f"wq{b}") for b in range(N // P)]
+        old0 = sb.tile([P, S], F32, name="old0")
+        nc.vector.tensor_copy(old0[:], store[0][:].indirect(slot_sb[:]))
+        xq = quantize(nc, sb, picked, S, "xq")
 
-        def product(y, b, xq):
+        w_grouped = sb.tile([P, N, PACK], BF16, name="w_grouped", align_bytes=64)
+        split = N - VECTOR_W_COLUMNS
+        nc.scalar.copy(
+            w_grouped[:, :split, :].rearrange("p (c i) j -> p c j i", i=4),
+            w_rows[:, :, :split].rearrange("p j (c i) -> p c j i", i=4),
+        )
+        nc.vector.tensor_copy(
+            w_grouped[:, split:, :].rearrange("p (c i) j -> p c j i", i=4),
+            w_rows[:, :, split:].rearrange("p j (c i) -> p c j i", i=4),
+        )
+        wq = quantize(nc, sb, w_grouped, N, "wq")
+        y = [psum.tile([P, S], F32, name=f"y{b}") for b in range(BLOCKS)]
+        for b in range(BLOCKS):
             nc.tensor.matmul_mx(
-                out=y,
-                lhsT=wq[b][0][:].bitcast(FP8X4),
-                lhsT_scale=wq[b][1][:],
+                out=y[b][:],
+                lhsT=wq[0][:, b * P : (b + 1) * P].bitcast(FP8X4),
+                lhsT_scale=wq[1][:, b * P : (b + 1) * P],
                 rhs=xq[0][:].bitcast(FP8X4),
                 rhs_scale=xq[1][:],
                 start=True,
                 stop=True,
             )
-
-        y0 = [psum.tile([P, HALF], F32, name=f"y0{h}") for h in range(2)]
-        y1 = psum.tile([P, S], F32, name="y1")
-        old0 = [sb.tile([P, HALF], F32, name=f"old0{h}", align_bytes=64) for h in range(2)]
-        new0 = [sb.tile([P, HALF], F32, name=f"new0{h}") for h in range(2)]
-        old1 = sb.tile([P, S], F32, name="old1")
-        new1 = sb.tile([P, S], F32, name="new1")
-
-        xq0_codes = sb.tile([P, HALF], U32, name="xq0_codes", align_bytes=64)
-        xq0_scales = sb.tile([P, HALF], U8, name="xq0_scales", align_bytes=64)
-        for c in range(0, HALF, HALF // 2):
-            cols = slice(c, c + HALF // 2)
-            nc.vector.quantize_mx(
-                out=xq0_codes[:, cols].bitcast(FP8X4),
-                scales=xq0_scales[:, cols],
-                in_=picked[0][:, cols, :].rearrange("p c j -> p (c j)"),
-            )
-        xq0 = (xq0_codes, xq0_scales)
-        product(y0[0][:], 0, xq0)
-        product(y1[:, 0:HALF], 1, xq0)
-        for h in range(2):
-            nc.vector.tensor_copy(old0[h][:], store[0][:].indirect(slot_half[h]))
-        nc.vector.tensor_tensor(new0[0][:], y0[0][:], old0[0][:], MIN)
-        nc.vector.tensor_copy(store[0][:].indirect(slot_half[0]), new0[0][:])
-        xq1 = quantize(nc, sb, picked[1], HALF, "xq1", tag="old00")
-        product(y0[1][:], 0, xq1)
-        product(y1[:, HALF:S], 1, xq1)
+        old1 = sb.tile([P, S], F32, name="old1", tag="picked", align_bytes=64)
         nc.vector.tensor_copy(old1[:], store[1][:].indirect(slot_sb[:]))
-        nc.vector.tensor_tensor(new0[1][:], y0[1][:], old0[1][:], MIN)
-        nc.vector.tensor_tensor(new1[:], y1[:], old1[:], MIN)
-        nc.vector.tensor_copy(store[0][:].indirect(slot_half[1]), new0[1][:])
-        nc.sync.dma_start(out[0:P, :], store[0][:])
-        nc.vector.tensor_copy(store[1][:].indirect(slot_sb[:]), new1[:])
-        nc.sync.dma_start(out[P : 2 * P, :], store[1][:])
+        old = [old0, old1]
+        new = [sb.tile([P, S], F32, name=f"new{b}") for b in range(BLOCKS)]
+        for b in range(BLOCKS):
+            nc.vector.tensor_tensor(new[b][:], y[b][:], old[b][:], MIN)
+        for b in range(BLOCKS):
+            nc.vector.tensor_copy(store[b][:].indirect(slot_sb[:]), new[b][:])
+            nc.sync.dma_start(out[b * P : (b + 1) * P, :], store[b][:])

@@ -20,7 +20,6 @@ LIST_ROWS = 16
 BLOCKS = N // P
 VECTOR_ENTRIES = 160
 FIRST_CAST = 704
-VECTOR_W_COLUMNS = 80
 
 
 def quantize(nc, pool, grouped, width, name):
@@ -69,34 +68,32 @@ def tile_picked_idxput_min_e_kernel(tc, xT, mem, w1, offs, slot, out):
         nc.vector.tensor_copy(old0[:], store[0][:].indirect(slot_sb[:]))
         xq = quantize(nc, sb, picked, S, "xq")
 
-        w_grouped = sb.tile([P, N, PACK], BF16, name="w_grouped", align_bytes=64)
-        split = N - VECTOR_W_COLUMNS
-        nc.scalar.copy(
-            w_grouped[:, :split, :].rearrange("p (c i) j -> p c j i", i=4),
-            w_rows[:, :, :split].rearrange("p j (c i) -> p c j i", i=4),
-        )
-        nc.vector.tensor_copy(
-            w_grouped[:, split:, :].rearrange("p (c i) j -> p c j i", i=4),
-            w_rows[:, :, split:].rearrange("p j (c i) -> p c j i", i=4),
-        )
-        wq = quantize(nc, sb, w_grouped, N, "wq")
-        y = [psum.tile([P, S], F32, name=f"y{b}") for b in range(BLOCKS)]
+        wq = []
         for b in range(BLOCKS):
-            nc.tensor.matmul_mx(
-                out=y[b][:],
-                lhsT=wq[0][:, b * P : (b + 1) * P].bitcast(FP8X4),
-                lhsT_scale=wq[1][:, b * P : (b + 1) * P],
-                rhs=xq[0][:].bitcast(FP8X4),
-                rhs_scale=xq[1][:],
-                start=True,
-                stop=True,
+            w_grouped = sb.tile([P, P, PACK], BF16, name=f"w_grouped{b}", align_bytes=64)
+            nc.scalar.copy(
+                w_grouped[:].rearrange("p (c i) j -> p c j i", i=4),
+                w_rows[:, :, b * P : (b + 1) * P].rearrange("p j (c i) -> p c j i", i=4),
             )
+            wq.append(quantize(nc, sb, w_grouped, P, f"wq{b}"))
+
         old1 = sb.tile([P, S], F32, name="old1", tag="picked", align_bytes=64)
         nc.vector.tensor_copy(old1[:], store[1][:].indirect(slot_sb[:]))
         old = [old0, old1]
         new = [sb.tile([P, S], F32, name=f"new{b}") for b in range(BLOCKS)]
-        for b in range(BLOCKS):
-            nc.vector.tensor_tensor(new[b][:], y[b][:], old[b][:], MIN)
+        for b, first, width in ((0, 0, S), (1, 0, S // 2), (1, S // 2, S // 2)):
+            cols = slice(first, first + width)
+            y = psum.tile([P, width], F32, name=f"y{b}_{first}")
+            nc.tensor.matmul_mx(
+                out=y[:],
+                lhsT=wq[b][0][:].bitcast(FP8X4),
+                lhsT_scale=wq[b][1][:],
+                rhs=xq[0][:, cols].bitcast(FP8X4),
+                rhs_scale=xq[1][:, cols],
+                start=True,
+                stop=True,
+            )
+            nc.vector.tensor_tensor(new[b][:, cols], y[:], old[b][:, cols], MIN)
         for b in range(BLOCKS):
             nc.vector.tensor_copy(store[b][:].indirect(slot_sb[:]), new[b][:])
             nc.sync.dma_start(out[b * P : (b + 1) * P, :], store[b][:])

@@ -38,9 +38,10 @@ def tile_picked_idxput_min_e_kernel(tc, xT, mem, w1, offs, slot, out):
         offs_sb = sb.tile([P, S // LIST_ROWS], U16, name="offs_sb")
         slot_sb = sb.tile([P, S // LIST_ROWS], U16, name="slot_sb")
         x_rows = [sb.tile([P, T], F32, name=f"x_rows{j}") for j in range(PACK)]
-        w_rows = sb.tile([P, PACK, N], F32, name="w_rows")
+        w_rows = [sb.tile([P, PACK, P], F32, name=f"w_rows{b}") for b in range(BLOCKS)]
         store = [sb.tile([P, U], F32, name=f"store{b}") for b in range(BLOCKS)]
 
+        w_by_row = w1.rearrange("(p j) m -> p j m", j=PACK)
         x_by_row = xT.rearrange("(p j) t -> p j t", j=PACK)
         nc.sync.dma_start(x_rows[0][:], x_by_row[:, 0, :])
         nc.sync.dma_start(offs_sb[:], offs)
@@ -49,8 +50,9 @@ def tile_picked_idxput_min_e_kernel(tc, xT, mem, w1, offs, slot, out):
         nc.sync.dma_start(x_rows[2][:], x_by_row[:, 2, :])
         nc.sync.dma_start(x_rows[3][:], x_by_row[:, 3, :])
         nc.sync.dma_start(store[0][:], mem[0:P, :])
-        nc.sync.dma_start(w_rows[:], w1.rearrange("(p j) m -> p j m", j=PACK))
+        nc.sync.dma_start(w_rows[0][:], w_by_row[:, :, 0 * P : 1 * P])
         nc.sync.dma_start(store[1][:], mem[P : 2 * P, :])
+        nc.sync.dma_start(w_rows[1][:], w_by_row[:, :, 1 * P : 2 * P])
 
         cut = VECTOR_ENTRIES // LIST_ROWS
         picked = sb.tile([P, S, PACK], BF16, name="picked", align_bytes=64)
@@ -73,14 +75,14 @@ def tile_picked_idxput_min_e_kernel(tc, xT, mem, w1, offs, slot, out):
             w_grouped = sb.tile([P, P, PACK], BF16, name=f"w_grouped{b}", align_bytes=64)
             nc.scalar.copy(
                 w_grouped[:].rearrange("p (c i) j -> p c j i", i=4),
-                w_rows[:, :, b * P : (b + 1) * P].rearrange("p j (c i) -> p c j i", i=4),
+                w_rows[b][:].rearrange("p j (c i) -> p c j i", i=4),
             )
             wq.append(quantize(nc, sb, w_grouped, P, f"wq{b}"))
 
         old1 = sb.tile([P, S], F32, name="old1", tag="picked", align_bytes=64)
         nc.vector.tensor_copy(old1[:], store[1][:].indirect(slot_sb[:]))
         old = [old0, old1]
-        new = [sb.tile([P, S], F32, name=f"new{b}") for b in range(BLOCKS)]
+        new = [sb.tile([P, S], F32, name="new0", tag="w_rows1"), sb.tile([P, S], F32, name="new1")]
         for b, first, width in ((0, 0, S), (1, 0, S // 2), (1, S // 2, S // 2)):
             cols = slice(first, first + width)
             y = psum.tile([P, width], F32, name=f"y{b}_{first}")

@@ -20,6 +20,8 @@ LIST_ROWS = 16
 BLOCKS = N // P
 VECTOR_ENTRIES = 160
 FIRST_CAST = 704
+FREE_MIN = 288
+FIRST_SCATTER = 320
 
 
 def quantize(nc, pool, grouped, width, name):
@@ -38,7 +40,9 @@ def tile_picked_idxput_min_e_kernel(tc, xT, mem, w1, offs, slot, out):
         offs_sb = sb.tile([P, S // LIST_ROWS], U16, name="offs_sb")
         slot_sb = sb.tile([P, S // LIST_ROWS], U16, name="slot_sb")
         x_rows = [sb.tile([P, T], F32, name=f"x_rows{j}") for j in range(PACK)]
-        w_rows = [sb.tile([P, PACK, P], F32, name=f"w_rows{b}") for b in range(BLOCKS)]
+        w_first = sb.tile([P, PACK, P], F32, name="w_first")
+        new0_w = sb.tile([P, FREE_MIN + PACK * P], F32, name="new0_w")
+        w_rows = [w_first[:], new0_w[:, FREE_MIN:].rearrange("p (j m) -> p j m", j=PACK)]
         store = [sb.tile([P, U], F32, name=f"store{b}") for b in range(BLOCKS)]
 
         w_by_row = w1.rearrange("(p j) m -> p j m", j=PACK)
@@ -50,9 +54,9 @@ def tile_picked_idxput_min_e_kernel(tc, xT, mem, w1, offs, slot, out):
         nc.sync.dma_start(x_rows[2][:], x_by_row[:, 2, :])
         nc.sync.dma_start(x_rows[3][:], x_by_row[:, 3, :])
         nc.sync.dma_start(store[0][:], mem[0:P, :])
-        nc.sync.dma_start(w_rows[0][:], w_by_row[:, :, 0 * P : 1 * P])
+        nc.sync.dma_start(w_rows[0], w_by_row[:, :, 0 * P : 1 * P])
         nc.sync.dma_start(store[1][:], mem[P : 2 * P, :])
-        nc.sync.dma_start(w_rows[1][:], w_by_row[:, :, 1 * P : 2 * P])
+        nc.sync.dma_start(w_rows[1], w_by_row[:, :, 1 * P : 2 * P])
 
         cut = VECTOR_ENTRIES // LIST_ROWS
         picked = sb.tile([P, S, PACK], BF16, name="picked", align_bytes=64)
@@ -75,15 +79,17 @@ def tile_picked_idxput_min_e_kernel(tc, xT, mem, w1, offs, slot, out):
             w_grouped = sb.tile([P, P, PACK], BF16, name=f"w_grouped{b}", align_bytes=64)
             nc.scalar.copy(
                 w_grouped[:].rearrange("p (c i) j -> p c j i", i=4),
-                w_rows[b][:].rearrange("p j (c i) -> p c j i", i=4),
+                w_rows[b].rearrange("p j (c i) -> p c j i", i=4),
             )
             wq.append(quantize(nc, sb, w_grouped, P, f"wq{b}"))
 
         old1 = sb.tile([P, S], F32, name="old1", tag="picked", align_bytes=64)
         nc.vector.tensor_copy(old1[:], store[1][:].indirect(slot_sb[:]))
         old = [old0, old1]
-        new = [sb.tile([P, S], F32, name="new0", tag="w_rows1"), sb.tile([P, S], F32, name="new1")]
-        for b, first, width in ((0, 0, S), (1, 0, S // 2), (1, S // 2, S // 2)):
+        new1 = sb.tile([P, S], F32, name="new1")
+        new = [new0_w, new1]
+
+        def product(b, first, width):
             cols = slice(first, first + width)
             y = psum.tile([P, width], F32, name=f"y{b}_{first}")
             nc.tensor.matmul_mx(
@@ -95,7 +101,19 @@ def tile_picked_idxput_min_e_kernel(tc, xT, mem, w1, offs, slot, out):
                 start=True,
                 stop=True,
             )
-            nc.vector.tensor_tensor(new[b][:, cols], y[:], old[b][:, cols], MIN)
-        for b in range(BLOCKS):
-            nc.vector.tensor_copy(store[b][:].indirect(slot_sb[:]), new[b][:])
-            nc.sync.dma_start(out[b * P : (b + 1) * P, :], store[b][:])
+            return y
+
+        def scatter(b, first, last):
+            entries = slot_sb[:, first // LIST_ROWS : last // LIST_ROWS]
+            nc.vector.tensor_copy(store[b][:].indirect(entries), new[b][:, first:last])
+
+        y0 = product(0, 0, S)
+        for first, last in ((0, FREE_MIN), (FREE_MIN, FIRST_SCATTER), (FIRST_SCATTER, S)):
+            nc.vector.tensor_tensor(new[0][:, first:last], y0[:, first:last], old[0][:, first:last], MIN)
+        scatter(0, 0, FIRST_SCATTER)
+        y1 = product(1, 0, S)
+        nc.vector.tensor_tensor(new[1][:], y1[:], old[1][:], MIN)
+        scatter(0, FIRST_SCATTER, S)
+        nc.sync.dma_start(out[0:P, :], store[0][:])
+        scatter(1, 0, S)
+        nc.sync.dma_start(out[P : 2 * P, :], store[1][:])

@@ -49,8 +49,8 @@ def tile_picked_idxput_min_e_kernel(tc, xT, mem, w1, offs, slot, out):
         x_by_row = xT.rearrange("(p j) t -> p j t", j=PACK)
         nc.sync.dma_start(x_rows[0][:], x_by_row[:, 0, :])
         nc.sync.dma_start(offs_sb[:], offs)
-        nc.sync.dma_start(slot_sb[:], slot)
         nc.sync.dma_start(x_rows[1][:], x_by_row[:, 1, :])
+        nc.sync.dma_start(slot_sb[:], slot)
         nc.sync.dma_start(x_rows[2][:], x_by_row[:, 2, :])
         nc.sync.dma_start(x_rows[3][:], x_by_row[:, 3, :])
         nc.sync.dma_start(store[0][:], mem[0:P, :])

@@ -20,8 +20,8 @@ LIST_ROWS = 16
 BLOCKS = N // P
 VECTOR_ENTRIES = 160
 FIRST_CAST = 704
-FREE_MIN = 288
-FIRST_SCATTER = 320
+FREE_MIN = 256
+FIRST_SCATTER = 288
 
 
 def quantize(nc, pool, grouped, width, name):
@@ -83,7 +83,7 @@ def tile_picked_idxput_min_e_kernel(tc, xT, mem, w1, offs, slot, out):
             )
             wq.append(quantize(nc, sb, w_grouped, P, f"wq{b}"))
 
-        old1 = sb.tile([P, S], F32, name="old1", tag="picked", align_bytes=64)
+        old1 = sb.tile([P, S], F32, name="old1", tag="w_first")
         nc.vector.tensor_copy(old1[:], store[1][:].indirect(slot_sb[:]))
         old = [old0, old1]
         new1 = sb.tile([P, S], F32, name="new1")

@@ -75,13 +75,15 @@ def tile_picked_idxput_min_e_kernel(tc, xT, mem, w1, offs, slot, out):
         xq = quantize(nc, sb, picked, S, "xq")
 
         wq = []
+        grouped = []
         for b in range(BLOCKS):
             w_grouped = sb.tile([P, P, PACK], BF16, name=f"w_grouped{b}", align_bytes=64)
             nc.scalar.copy(
                 w_grouped[:].rearrange("p (c i) j -> p c j i", i=4),
                 w_rows[b].rearrange("p j (c i) -> p c j i", i=4),
             )
-            wq.append(quantize(nc, sb, w_grouped, P, f"wq{b}"))
+            grouped.append(w_grouped)
+        wq.append(quantize(nc, sb, grouped[0], P, "wq0"))
 
         old1 = sb.tile([P, S], F32, name="old1", tag="w_first")
         nc.vector.tensor_copy(old1[:], store[1][:].indirect(slot_sb[:]))
@@ -109,6 +111,8 @@ def tile_picked_idxput_min_e_kernel(tc, xT, mem, w1, offs, slot, out):
 
         y0 = product(0, 0, S)
         for first, last in ((0, FREE_MIN), (FREE_MIN, FIRST_SCATTER), (FIRST_SCATTER, S)):
+            if first == FIRST_SCATTER:
+                wq.append(quantize(nc, sb, grouped[1], P, "wq1"))
             nc.vector.tensor_tensor(new[0][:, first:last], y0[:, first:last], old[0][:, first:last], MIN)
         scatter(0, 0, FIRST_SCATTER)
         y1 = product(1, 0, S)

@@ -12,7 +12,11 @@ U16 = mybir.dt.uint16
 U8 = mybir.dt.uint8
 FP8X4 = mybir.dt.float8_e4m3fn_x4
 COPY = mybir.ActivationFunctionType.Copy
+SIGN = mybir.ActivationFunctionType.Sign
 MIN = mybir.AluOpType.min
+ADD = mybir.AluOpType.add
+SUB = mybir.AluOpType.subtract
+MULT = mybir.AluOpType.mult
 
 P = 128
 PACK = 4
@@ -20,8 +24,10 @@ LIST_ROWS = 16
 BLOCKS = N // P
 VECTOR_ENTRIES = 160
 FIRST_CAST = 704
-FREE_MIN = 256
-FIRST_SCATTER = 288
+FREE_MIN = 224
+FIRST_SCATTER = 256
+SECOND_SCATTER = 384
+MASKED = 256
 
 
 def quantize(nc, pool, grouped, width, name):
@@ -88,7 +94,7 @@ def tile_picked_idxput_min_e_kernel(tc, xT, mem, w1, offs, slot, out):
         old1 = sb.tile([P, S], F32, name="old1", tag="w_first")
         nc.vector.tensor_copy(old1[:], store[1][:].indirect(slot_sb[:]))
         old = [old0, old1]
-        new1 = sb.tile([P, S], F32, name="new1")
+        new1 = sb.tile([P, S - MASKED], F32, name="new1")
         new = [new0_w, new1]
 
         def product(b, first, width):
@@ -115,9 +121,29 @@ def tile_picked_idxput_min_e_kernel(tc, xT, mem, w1, offs, slot, out):
                 wq.append(quantize(nc, sb, grouped[1], P, "wq1"))
             nc.vector.tensor_tensor(new[0][:, first:last], y0[:, first:last], old[0][:, first:last], MIN)
         scatter(0, 0, FIRST_SCATTER)
-        y1 = product(1, 0, S)
-        nc.vector.tensor_tensor(new[1][:], y1[:], old[1][:], MIN)
-        scatter(0, FIRST_SCATTER, S)
+        plain = S - MASKED
+        y1 = product(1, 0, plain)
+        y1_late = product(1, plain, MASKED)
+        nc.vector.tensor_tensor(new[1][:, :plain], y1[:], old[1][:, :plain], MIN)
+
+        y_late = sb.tile([P, MASKED], F32, name="y_late")
+        diff = sb.tile([P, MASKED], F32, name="diff")
+        sign = sb.tile([P, MASKED], F32, name="sign")
+        take_y = sb.tile([P, MASKED], F32, name="take_y")
+        take_old = sb.tile([P, MASKED], F32, name="take_old")
+        part_y = sb.tile([P, MASKED], F32, name="part_y")
+        part_old = sb.tile([P, MASKED], F32, name="part_old")
+        nc.scalar.copy(y_late[:], y1_late[:])
+        nc.gpsimd.tensor_tensor(diff[:], old[1][:, plain:], y_late[:], SUB)
+        nc.scalar.activation(sign[:], diff[:], SIGN)
+        nc.scalar.activation(take_y[:], sign[:], COPY, bias=0.5, scale=0.5)
+        nc.scalar.activation(take_old[:], sign[:], COPY, bias=0.5, scale=-0.5)
+        nc.gpsimd.tensor_tensor(part_y[:], y_late[:], take_y[:], MULT)
+        nc.gpsimd.tensor_tensor(part_old[:], old[1][:, plain:], take_old[:], MULT)
+
+        scatter(0, FIRST_SCATTER, SECOND_SCATTER)
+        scatter(1, 0, plain)
+        scatter(0, SECOND_SCATTER, S)
         nc.sync.dma_start(out[0:P, :], store[0][:])
-        scatter(1, 0, S)
+        nc.vector.tensor_tensor(store[1][:].indirect(slot_sb[:, plain // LIST_ROWS :]), part_y[:], part_old[:], ADD)
         nc.sync.dma_start(out[P : 2 * P, :], store[1][:])

@@ -27,7 +27,7 @@ FIRST_CAST = 704
 FREE_MIN = 224
 FIRST_SCATTER = 256
 SECOND_SCATTER = 384
-MASKED = 256
+MASKED = 192
 
 
 def quantize(nc, pool, grouped, width, name):
@@ -97,33 +97,36 @@ def tile_picked_idxput_min_e_kernel(tc, xT, mem, w1, offs, slot, out):
         new1 = sb.tile([P, S - MASKED], F32, name="new1")
         new = [new0_w, new1]
 
-        def product(b, first, width):
-            cols = slice(first, first + width)
-            y = psum.tile([P, width], F32, name=f"y{b}_{first}")
-            nc.tensor.matmul_mx(
-                out=y[:],
-                lhsT=wq[b][0][:].bitcast(FP8X4),
-                lhsT_scale=wq[b][1][:],
-                rhs=xq[0][:, cols].bitcast(FP8X4),
-                rhs_scale=xq[1][:, cols],
-                start=True,
-                stop=True,
-            )
+        def product(b, first, widths):
+            y = psum.tile([P, sum(widths)], F32, name=f"y{b}_{first}")
+            done = 0
+            for width in widths:
+                cols = slice(first + done, first + done + width)
+                nc.tensor.matmul_mx(
+                    out=y[:, done : done + width],
+                    lhsT=wq[b][0][:].bitcast(FP8X4),
+                    lhsT_scale=wq[b][1][:],
+                    rhs=xq[0][:, cols].bitcast(FP8X4),
+                    rhs_scale=xq[1][:, cols],
+                    start=True,
+                    stop=True,
+                )
+                done = done + width
             return y
 
         def scatter(b, first, last):
             entries = slot_sb[:, first // LIST_ROWS : last // LIST_ROWS]
             nc.vector.tensor_copy(store[b][:].indirect(entries), new[b][:, first:last])
 
-        y0 = product(0, 0, S)
+        y0 = product(0, 0, [S])
         for first, last in ((0, FREE_MIN), (FREE_MIN, FIRST_SCATTER), (FIRST_SCATTER, S)):
             if first == FIRST_SCATTER:
                 wq.append(quantize(nc, sb, grouped[1], P, "wq1"))
             nc.vector.tensor_tensor(new[0][:, first:last], y0[:, first:last], old[0][:, first:last], MIN)
         scatter(0, 0, FIRST_SCATTER)
         plain = S - MASKED
-        y1 = product(1, 0, plain)
-        y1_late = product(1, plain, MASKED)
+        y1 = product(1, 0, [256, 64])
+        y1_late = product(1, plain, [128, 64])
         nc.vector.tensor_tensor(new[1][:, :plain], y1[:], old[1][:, :plain], MIN)
 
         y_late = sb.tile([P, MASKED], F32, name="y_late")

@@ -26,8 +26,7 @@ VECTOR_ENTRIES = 160
 FIRST_CAST = 704
 FREE_MIN = 224
 FIRST_SCATTER = 256
-SECOND_SCATTER = 384
-MASKED = 192
+MASKED = (128, 192)
 
 
 def quantize(nc, pool, grouped, width, name):
@@ -47,8 +46,9 @@ def tile_picked_idxput_min_e_kernel(tc, xT, mem, w1, offs, slot, out):
         slot_sb = sb.tile([P, S // LIST_ROWS], U16, name="slot_sb")
         x_rows = [sb.tile([P, T], F32, name=f"x_rows{j}") for j in range(PACK)]
         w_first = sb.tile([P, PACK, P], F32, name="w_first")
-        new0_w = sb.tile([P, FREE_MIN + PACK * P], F32, name="new0_w")
-        w_rows = [w_first[:], new0_w[:, FREE_MIN:].rearrange("p (j m) -> p j m", j=PACK)]
+        work0 = sb.tile([P, S + PACK * P + FREE_MIN], F32, name="work0")
+        w_end = S + PACK * P
+        w_rows = [w_first[:], work0[:, S:w_end].rearrange("p (j m) -> p j m", j=PACK)]
         store = [sb.tile([P, U], F32, name=f"store{b}") for b in range(BLOCKS)]
 
         w_by_row = w1.rearrange("(p j) m -> p j m", j=PACK)
@@ -76,8 +76,7 @@ def tile_picked_idxput_min_e_kernel(tc, xT, mem, w1, offs, slot, out):
             nc.vector.tensor_copy(picked[:, :VECTOR_ENTRIES, j], x_rows[j][:].indirect(offs_sb[:, :cut]))
             nc.scalar.activation(picked[:, VECTOR_ENTRIES:, j], x_bf[:].indirect(offs_sb[:, cut:]), COPY)
 
-        old0 = sb.tile([P, S], F32, name="old0")
-        nc.vector.tensor_copy(old0[:], store[0][:].indirect(slot_sb[:]))
+        nc.vector.tensor_copy(work0[:, :S], store[0][:].indirect(slot_sb[:]))
         xq = quantize(nc, sb, picked, S, "xq")
 
         wq = []
@@ -91,11 +90,10 @@ def tile_picked_idxput_min_e_kernel(tc, xT, mem, w1, offs, slot, out):
             grouped.append(w_grouped)
         wq.append(quantize(nc, sb, grouped[0], P, "wq0"))
 
-        old1 = sb.tile([P, S], F32, name="old1", tag="w_first")
-        nc.vector.tensor_copy(old1[:], store[1][:].indirect(slot_sb[:]))
-        old = [old0, old1]
-        new1 = sb.tile([P, S - MASKED], F32, name="new1")
-        new = [new0_w, new1]
+        old1 = sb.tile([P, S + MASKED[1]], F32, name="old1", tag="w_first")
+        nc.vector.tensor_copy(old1[:, :S], store[1][:].indirect(slot_sb[:]))
+        old = [work0, old1]
+        new1 = sb.tile([P, S - MASKED[1]], F32, name="new1")
 
         def product(b, first, widths):
             y = psum.tile([P, sum(widths)], F32, name=f"y{b}_{first}")
@@ -114,39 +112,49 @@ def tile_picked_idxput_min_e_kernel(tc, xT, mem, w1, offs, slot, out):
                 done = done + width
             return y
 
-        def scatter(b, first, last):
+        def scatter(b, first, last, values):
             entries = slot_sb[:, first // LIST_ROWS : last // LIST_ROWS]
-            nc.vector.tensor_copy(store[b][:].indirect(entries), new[b][:, first:last])
+            nc.vector.tensor_copy(store[b][:].indirect(entries), values)
 
-        y0 = product(0, 0, [S])
-        for first, last in ((0, FREE_MIN), (FREE_MIN, FIRST_SCATTER), (FIRST_SCATTER, S)):
-            if first == FIRST_SCATTER:
-                wq.append(quantize(nc, sb, grouped[1], P, "wq1"))
-            nc.vector.tensor_tensor(new[0][:, first:last], y0[:, first:last], old[0][:, first:last], MIN)
-        scatter(0, 0, FIRST_SCATTER)
-        plain = S - MASKED
+        def masked_parts(b, y, diff_tag):
+            count = MASKED[b]
+            both = old[b][:, S - count : S + count]
+            diff = sb.tile([P, count], F32, name=f"diff{b}", tag=diff_tag, align_bytes=64)
+            sign = sb.tile([P, count], F32, name=f"sign{b}")
+            take = sb.tile([P, 2 * count], F32, name=f"take{b}")
+            parts = sb.tile([P, 2 * count], F32, name=f"parts{b}")
+            nc.scalar.copy(both[:, count:], y)
+            nc.gpsimd.tensor_tensor(diff[:], both[:, :count], both[:, count:], SUB)
+            nc.scalar.activation(sign[:], diff[:], SIGN)
+            nc.scalar.activation(take[:, :count], sign[:], COPY, bias=0.5, scale=-0.5)
+            nc.scalar.activation(take[:, count:], sign[:], COPY, bias=0.5, scale=0.5)
+            nc.gpsimd.tensor_tensor(parts[:], both, take[:], MULT)
+            return parts[:, :count], parts[:, count:]
+
+        plain = [S - count for count in MASKED]
+        held = FIRST_SCATTER - FREE_MIN
+        cover = plain[0] - FIRST_SCATTER
+        first_new = work0[:, w_end - held :]
+        cover_new = work0[:, w_end - held - cover : w_end - held]
+        late_new = work0[:, S + MASKED[0] : S + 2 * MASKED[0]]
+        y0 = product(0, 0, [256, 128])
+        y0_late = product(0, plain[0], [128])
+        nc.vector.tensor_tensor(first_new[:, held:], y0[:, held:FIRST_SCATTER], work0[:, held:FIRST_SCATTER], MIN)
+        nc.vector.tensor_tensor(first_new[:, :held], y0[:, :held], work0[:, :held], MIN)
+        wq.append(quantize(nc, sb, grouped[1], P, "wq1"))
+        nc.vector.tensor_tensor(cover_new, y0[:, FIRST_SCATTER:], work0[:, FIRST_SCATTER : plain[0]], MIN)
+        scatter(0, 0, FIRST_SCATTER, first_new)
         y1 = product(1, 0, [256, 64])
-        y1_late = product(1, plain, [128, 64])
-        nc.vector.tensor_tensor(new[1][:, :plain], y1[:], old[1][:, :plain], MIN)
+        y1_late = product(1, plain[1], [128, 64])
+        nc.vector.tensor_tensor(new1[:], y1[:], old1[:, : plain[1]], MIN)
 
-        y_late = sb.tile([P, MASKED], F32, name="y_late")
-        diff = sb.tile([P, MASKED], F32, name="diff")
-        sign = sb.tile([P, MASKED], F32, name="sign")
-        take_y = sb.tile([P, MASKED], F32, name="take_y")
-        take_old = sb.tile([P, MASKED], F32, name="take_old")
-        part_y = sb.tile([P, MASKED], F32, name="part_y")
-        part_old = sb.tile([P, MASKED], F32, name="part_old")
-        nc.scalar.copy(y_late[:], y1_late[:])
-        nc.gpsimd.tensor_tensor(diff[:], old[1][:, plain:], y_late[:], SUB)
-        nc.scalar.activation(sign[:], diff[:], SIGN)
-        nc.scalar.activation(take_y[:], sign[:], COPY, bias=0.5, scale=0.5)
-        nc.scalar.activation(take_old[:], sign[:], COPY, bias=0.5, scale=-0.5)
-        nc.gpsimd.tensor_tensor(part_y[:], y_late[:], take_y[:], MULT)
-        nc.gpsimd.tensor_tensor(part_old[:], old[1][:, plain:], take_old[:], MULT)
+        parts0 = masked_parts(0, y0_late[:], "w_grouped1")
+        nc.gpsimd.tensor_tensor(late_new, parts0[0], parts0[1], ADD)
+        parts1 = masked_parts(1, y1_late[:], "diff1")
 
-        scatter(0, FIRST_SCATTER, SECOND_SCATTER)
-        scatter(1, 0, plain)
-        scatter(0, SECOND_SCATTER, S)
+        scatter(0, FIRST_SCATTER, plain[0], cover_new)
+        scatter(1, 0, plain[1], new1[:])
+        scatter(0, plain[0], S, late_new)
         nc.sync.dma_start(out[0:P, :], store[0][:])
-        nc.vector.tensor_tensor(store[1][:].indirect(slot_sb[:, plain // LIST_ROWS :]), part_y[:], part_old[:], ADD)
+        nc.vector.tensor_tensor(store[1][:].indirect(slot_sb[:, plain[1] // LIST_ROWS :]), parts1[0], parts1[1], ADD)
         nc.sync.dma_start(out[P : 2 * P, :], store[1][:])

@@ -12,28 +12,19 @@ U16 = mybir.dt.uint16
 U8 = mybir.dt.uint8
 FP8X4 = mybir.dt.float8_e4m3fn_x4
 COPY = mybir.ActivationFunctionType.Copy
-SIGN = mybir.ActivationFunctionType.Sign
 MIN = mybir.AluOpType.min
-ADD = mybir.AluOpType.add
-SUB = mybir.AluOpType.subtract
-MULT = mybir.AluOpType.mult
 
 P = 128
 PACK = 4
 LIST_ROWS = 16
-BLOCKS = N // P
-VECTOR_ENTRIES = 160
-FIRST_CAST = 704
-FREE_MIN = 224
-FIRST_SCATTER = 256
-MASKED = (128, 192)
+HALF = S // 2
+QUARTER = S // 4
+WEAVE_SCALAR = 64
+LATE_SCATTER = 288
 
 
-def quantize(nc, pool, grouped, width, name):
-    codes = pool.tile([P, width], U32, name=name + "_codes", align_bytes=64)
-    scales = pool.tile([P, width], U8, name=name + "_scales", align_bytes=64)
-    nc.vector.quantize_mx(out=codes[:].bitcast(FP8X4), scales=scales[:], in_=grouped[:].rearrange("p c j -> p (c j)"))
-    return codes, scales
+def entries(index_tile, first, last):
+    return index_tile[:, first // LIST_ROWS : last // LIST_ROWS]
 
 
 def tile_picked_idxput_min_e_kernel(tc, xT, mem, w1, offs, slot, out):
@@ -45,14 +36,12 @@ def tile_picked_idxput_min_e_kernel(tc, xT, mem, w1, offs, slot, out):
         offs_sb = sb.tile([P, S // LIST_ROWS], U16, name="offs_sb")
         slot_sb = sb.tile([P, S // LIST_ROWS], U16, name="slot_sb")
         x_rows = [sb.tile([P, T], F32, name=f"x_rows{j}") for j in range(PACK)]
-        w_first = sb.tile([P, PACK, P], F32, name="w_first")
-        work0 = sb.tile([P, S + PACK * P + FREE_MIN], F32, name="work0")
-        w_end = S + PACK * P
-        w_rows = [w_first[:], work0[:, S:w_end].rearrange("p (j m) -> p j m", j=PACK)]
-        store = [sb.tile([P, U], F32, name=f"store{b}") for b in range(BLOCKS)]
+        w_rows = [sb.tile([P, PACK, P], F32, name=f"w_rows{b}") for b in range(2)]
+        store = [sb.tile([P, U], F32, name=f"store{b}") for b in range(2)]
 
-        w_by_row = w1.rearrange("(p j) m -> p j m", j=PACK)
         x_by_row = xT.rearrange("(p j) t -> p j t", j=PACK)
+        w_by_row = w1.rearrange("(p j) m -> p j m", j=PACK)
+        nc.sync.dma_start(w_rows[0][:], w_by_row[:, :, :P])
         nc.sync.dma_start(x_rows[0][:], x_by_row[:, 0, :])
         nc.sync.dma_start(offs_sb[:], offs)
         nc.sync.dma_start(x_rows[1][:], x_by_row[:, 1, :])
@@ -60,101 +49,102 @@ def tile_picked_idxput_min_e_kernel(tc, xT, mem, w1, offs, slot, out):
         nc.sync.dma_start(x_rows[2][:], x_by_row[:, 2, :])
         nc.sync.dma_start(x_rows[3][:], x_by_row[:, 3, :])
         nc.sync.dma_start(store[0][:], mem[0:P, :])
-        nc.sync.dma_start(w_rows[0], w_by_row[:, :, 0 * P : 1 * P])
+        nc.sync.dma_start(w_rows[1][:], w_by_row[:, :, P:])
         nc.sync.dma_start(store[1][:], mem[P : 2 * P, :])
-        nc.sync.dma_start(w_rows[1], w_by_row[:, :, 1 * P : 2 * P])
 
-        cut = VECTOR_ENTRIES // LIST_ROWS
-        picked = sb.tile([P, S, PACK], BF16, name="picked", align_bytes=64)
-        for j in range(PACK):
-            x_bf = sb.tile([P, T], BF16, name=f"x_bf{j}")
-            if j == 0:
-                nc.vector.tensor_copy(x_bf[:, :FIRST_CAST], x_rows[j][:, :FIRST_CAST])
-                nc.scalar.copy(x_bf[:, FIRST_CAST:], x_rows[j][:, FIRST_CAST:])
-            else:
-                nc.vector.tensor_copy(x_bf[:], x_rows[j][:])
-            nc.vector.tensor_copy(picked[:, :VECTOR_ENTRIES, j], x_rows[j][:].indirect(offs_sb[:, :cut]))
-            nc.scalar.activation(picked[:, VECTOR_ENTRIES:, j], x_bf[:].indirect(offs_sb[:, cut:]), COPY)
-
-        nc.vector.tensor_copy(work0[:, :S], store[0][:].indirect(slot_sb[:]))
-        xq = quantize(nc, sb, picked, S, "xq")
-
-        wq = []
-        grouped = []
-        for b in range(BLOCKS):
-            w_grouped = sb.tile([P, P, PACK], BF16, name=f"w_grouped{b}", align_bytes=64)
-            nc.scalar.copy(
-                w_grouped[:].rearrange("p (c i) j -> p c j i", i=4),
-                w_rows[b].rearrange("p j (c i) -> p c j i", i=4),
+        def weave(copy, grouped, rows, first, last):
+            copy(
+                grouped[:, first:last, :].rearrange("p (c i) j -> p c j i", i=4),
+                rows[:, :, first:last].rearrange("p j (c i) -> p c j i", i=4),
             )
-            grouped.append(w_grouped)
-        wq.append(quantize(nc, sb, grouped[0], P, "wq0"))
 
-        old1 = sb.tile([P, S + MASKED[1]], F32, name="old1", tag="w_first")
-        nc.vector.tensor_copy(old1[:, :S], store[1][:].indirect(slot_sb[:]))
-        old = [work0, old1]
-        new1 = sb.tile([P, S - MASKED[1]], F32, name="new1")
+        def quantize(codes, scales, grouped):
+            nc.vector.quantize_mx(out=codes.bitcast(FP8X4), scales=scales, in_=grouped.rearrange("p c j -> p (c j)"))
 
-        def product(b, first, widths):
-            y = psum.tile([P, sum(widths)], F32, name=f"y{b}_{first}")
-            done = 0
-            for width in widths:
-                cols = slice(first + done, first + done + width)
-                nc.tensor.matmul_mx(
-                    out=y[:, done : done + width],
-                    lhsT=wq[b][0][:].bitcast(FP8X4),
-                    lhsT_scale=wq[b][1][:],
-                    rhs=xq[0][:, cols].bitcast(FP8X4),
-                    rhs_scale=xq[1][:, cols],
-                    start=True,
-                    stop=True,
-                )
-                done = done + width
-            return y
+        w_grouped = [sb.tile([P, P, PACK], BF16, name=f"w_grouped{b}", align_bytes=64) for b in range(2)]
+        w_codes = [sb.tile([P, P], U32, name=f"w_codes{b}", align_bytes=64) for b in range(2)]
+        w_scales = [sb.tile([P, P], U8, name=f"w_scales{b}", align_bytes=64) for b in range(2)]
+        weave(nc.scalar.copy, w_grouped[0], w_rows[0], 0, P)
+        quantize(w_codes[0][:], w_scales[0][:], w_grouped[0][:])
 
-        def scatter(b, first, last, values):
-            entries = slot_sb[:, first // LIST_ROWS : last // LIST_ROWS]
-            nc.vector.tensor_copy(store[b][:].indirect(entries), values)
+        woven = sb.tile([P, HALF, PACK], BF16, name="woven", align_bytes=64)
+        planes = sb.tile([P, PACK, HALF], BF16, name="planes")
+        both = sb.tile([P, HALF, PACK], BF16, name="both", align_bytes=64)
+        for j in range(PACK):
+            nc.scalar.activation(planes[:, j, :], x_rows[j][:].indirect(entries(offs_sb, 0, HALF)), COPY)
+            if j < PACK - 1:
+                nc.vector.tensor_copy(both[:, :, j], x_rows[j][:].indirect(entries(offs_sb, HALF, S)))
+            else:
+                for first in (0, QUARTER):
+                    picks = entries(offs_sb, HALF + first, HALF + first + QUARTER)
+                    nc.vector.tensor_copy(both[:, first : first + QUARTER, j], x_rows[j][:].indirect(picks))
+        weave(nc.scalar.copy, woven, planes, 0, WEAVE_SCALAR)
+        weave(nc.vector.tensor_copy, woven, planes, WEAVE_SCALAR, HALF)
 
-        def masked_parts(b, y, diff_tag):
-            count = MASKED[b]
-            both = old[b][:, S - count : S + count]
-            diff = sb.tile([P, count], F32, name=f"diff{b}", tag=diff_tag, align_bytes=64)
-            sign = sb.tile([P, count], F32, name=f"sign{b}")
-            take = sb.tile([P, 2 * count], F32, name=f"take{b}")
-            parts = sb.tile([P, 2 * count], F32, name=f"parts{b}")
-            nc.scalar.copy(both[:, count:], y)
-            nc.gpsimd.tensor_tensor(diff[:], both[:, :count], both[:, count:], SUB)
-            nc.scalar.activation(sign[:], diff[:], SIGN)
-            nc.scalar.activation(take[:, :count], sign[:], COPY, bias=0.5, scale=-0.5)
-            nc.scalar.activation(take[:, count:], sign[:], COPY, bias=0.5, scale=0.5)
-            nc.gpsimd.tensor_tensor(parts[:], both, take[:], MULT)
-            return parts[:, :count], parts[:, count:]
+        x_codes = sb.tile([P, S], U32, name="x_codes", align_bytes=64)
+        x_scales = sb.tile([P, S], U8, name="x_scales", align_bytes=64)
+        for first in (0, QUARTER):
+            cols = slice(HALF + first, HALF + first + QUARTER)
+            quantize(x_codes[:, cols], x_scales[:, cols], both[:, first : first + QUARTER, :])
+        quantize(x_codes[:, :HALF], x_scales[:, :HALF], woven[:])
 
-        plain = [S - count for count in MASKED]
-        held = FIRST_SCATTER - FREE_MIN
-        cover = plain[0] - FIRST_SCATTER
-        first_new = work0[:, w_end - held :]
-        cover_new = work0[:, w_end - held - cover : w_end - held]
-        late_new = work0[:, S + MASKED[0] : S + 2 * MASKED[0]]
-        y0 = product(0, 0, [256, 128])
-        y0_late = product(0, plain[0], [128])
-        nc.vector.tensor_tensor(first_new[:, held:], y0[:, held:FIRST_SCATTER], work0[:, held:FIRST_SCATTER], MIN)
-        nc.vector.tensor_tensor(first_new[:, :held], y0[:, :held], work0[:, :held], MIN)
-        wq.append(quantize(nc, sb, grouped[1], P, "wq1"))
-        nc.vector.tensor_tensor(cover_new, y0[:, FIRST_SCATTER:], work0[:, FIRST_SCATTER : plain[0]], MIN)
-        scatter(0, 0, FIRST_SCATTER, first_new)
-        y1 = product(1, 0, [256, 64])
-        y1_late = product(1, plain[1], [128, 64])
-        nc.vector.tensor_tensor(new1[:], y1[:], old1[:, : plain[1]], MIN)
+        def product(y, b, first, width):
+            cols = slice(first, first + width)
+            nc.tensor.matmul_mx(
+                out=y,
+                lhsT=w_codes[b][:].bitcast(FP8X4),
+                lhsT_scale=w_scales[b][:],
+                rhs=x_codes[:, cols].bitcast(FP8X4),
+                rhs_scale=x_scales[:, cols],
+                start=True,
+                stop=True,
+            )
 
-        parts0 = masked_parts(0, y0_late[:], "w_grouped1")
-        nc.gpsimd.tensor_tensor(late_new, parts0[0], parts0[1], ADD)
-        parts1 = masked_parts(1, y1_late[:], "diff1")
+        old = sb.tile([P, 2 * S], F32, name="old")
+        new = sb.tile([P, 2 * S], F32, name="new")
+        base = (S, 0)
 
-        scatter(0, FIRST_SCATTER, plain[0], cover_new)
-        scatter(1, 0, plain[1], new1[:])
-        scatter(0, plain[0], S, late_new)
+        def look_up(engine, b, first, last):
+            window = store[b][:].indirect(entries(slot_sb, first, last))
+            if engine is nc.vector:
+                nc.vector.tensor_copy(old[:, base[b] + first : base[b] + last], window)
+            else:
+                nc.scalar.activation(old[:, base[b] + first : base[b] + last], window, COPY)
+
+        def scatter(engine, b, first, last):
+            window = store[b][:].indirect(entries(slot_sb, first, last))
+            if engine is nc.vector:
+                nc.vector.tensor_copy(window, new[:, base[b] + first : base[b] + last])
+            else:
+                nc.scalar.activation(window, new[:, base[b] + first : base[b] + last], COPY)
+
+        def minimum(y, first, last):
+            nc.vector.tensor_tensor(new[:, first:last], y, old[:, first:last], MIN)
+
+        y_early = psum.tile([P, HALF], F32, name="y_early")
+        y_lead = psum.tile([P, QUARTER], F32, name="y_lead")
+        y_joint = psum.tile([P, QUARTER + HALF], F32, name="y_joint")
+        y_rest = psum.tile([P, HALF], F32, name="y_rest")
+
+        product(y_early[:], 0, HALF, HALF)
+        look_up(nc.scalar, 0, HALF, S)
+        look_up(nc.scalar, 0, 0, HALF)
+        weave(nc.vector.tensor_copy, w_grouped[1], w_rows[1], 0, P)
+        minimum(y_early[:], S + HALF, 2 * S)
+        quantize(w_codes[1][:], w_scales[1][:], w_grouped[1][:])
+        product(y_joint[:, QUARTER:], 0, 0, HALF)
+        product(y_lead[:], 1, 0, QUARTER)
+        product(y_joint[:, :QUARTER], 1, S - QUARTER, QUARTER)
+        product(y_rest[:], 1, QUARTER, HALF)
+
+        scatter(nc.scalar, 0, LATE_SCATTER, S)
+        look_up(nc.vector, 1, 0, QUARTER)
+        look_up(nc.vector, 1, QUARTER, S)
+        minimum(y_lead[:], 0, QUARTER)
+        scatter(nc.scalar, 1, 0, QUARTER)
+        minimum(y_joint[:], S - QUARTER, S + HALF)
+        minimum(y_rest[:], QUARTER, S - QUARTER)
+        scatter(nc.vector, 0, 0, LATE_SCATTER)
         nc.sync.dma_start(out[0:P, :], store[0][:])
-        nc.vector.tensor_tensor(store[1][:].indirect(slot_sb[:, plain[1] // LIST_ROWS :]), parts1[0], parts1[1], ADD)
+        scatter(nc.scalar, 1, QUARTER, S)
         nc.sync.dma_start(out[P : 2 * P, :], store[1][:])

@@ -19,8 +19,8 @@ PACK = 4
 LIST_ROWS = 16
 HALF = S // 2
 QUARTER = S // 4
-WEAVE_SCALAR = 64
-LATE_SCATTER = 288
+LATE_SCATTER = 352
+OLD1_SCALAR = 128
 
 
 def entries(index_tile, first, last):
@@ -67,26 +67,21 @@ def tile_picked_idxput_min_e_kernel(tc, xT, mem, w1, offs, slot, out):
         weave(nc.scalar.copy, w_grouped[0], w_rows[0], 0, P)
         quantize(w_codes[0][:], w_scales[0][:], w_grouped[0][:])
 
-        woven = sb.tile([P, HALF, PACK], BF16, name="woven", align_bytes=64)
-        planes = sb.tile([P, PACK, HALF], BF16, name="planes")
-        both = sb.tile([P, HALF, PACK], BF16, name="both", align_bytes=64)
+        picked = sb.tile([P, S, PACK], BF16, name="picked", align_bytes=64)
+        planes = [sb.tile([P, 2, QUARTER], BF16, name=f"planes{u}") for u in range(2)]
         for j in range(PACK):
-            nc.scalar.activation(planes[:, j, :], x_rows[j][:].indirect(entries(offs_sb, 0, HALF)), COPY)
-            if j < PACK - 1:
-                nc.vector.tensor_copy(both[:, :, j], x_rows[j][:].indirect(entries(offs_sb, HALF, S)))
-            else:
-                for first in (0, QUARTER):
-                    picks = entries(offs_sb, HALF + first, HALF + first + QUARTER)
-                    nc.vector.tensor_copy(both[:, first : first + QUARTER, j], x_rows[j][:].indirect(picks))
-        weave(nc.scalar.copy, woven, planes, 0, WEAVE_SCALAR)
-        weave(nc.vector.tensor_copy, woven, planes, WEAVE_SCALAR, HALF)
+            u = j // 2
+            nc.scalar.activation(planes[u][:, j % 2, :], x_rows[j][:].indirect(entries(offs_sb, 0, QUARTER)), COPY)
+            if j % 2 == 1:
+                nc.scalar.copy(picked[:, :QUARTER, 2 * u : 2 * u + 2], planes[u][:].rearrange("p j c -> p c j"))
+            pieces = [(QUARTER, S)] if j < PACK - 1 else [(HALF, S), (QUARTER, HALF)]
+            for first, last in pieces:
+                nc.vector.tensor_copy(picked[:, first:last, j], x_rows[j][:].indirect(entries(offs_sb, first, last)))
 
         x_codes = sb.tile([P, S], U32, name="x_codes", align_bytes=64)
         x_scales = sb.tile([P, S], U8, name="x_scales", align_bytes=64)
-        for first in (0, QUARTER):
-            cols = slice(HALF + first, HALF + first + QUARTER)
-            quantize(x_codes[:, cols], x_scales[:, cols], both[:, first : first + QUARTER, :])
-        quantize(x_codes[:, :HALF], x_scales[:, :HALF], woven[:])
+        for cols in (slice(HALF, S), slice(0, HALF)):
+            quantize(x_codes[:, cols], x_scales[:, cols], picked[:, cols, :])
 
         def product(y, b, first, width):
             cols = slice(first, first + width)
@@ -128,18 +123,19 @@ def tile_picked_idxput_min_e_kernel(tc, xT, mem, w1, offs, slot, out):
 
         product(y_early[:], 0, HALF, HALF)
         look_up(nc.scalar, 0, HALF, S)
-        look_up(nc.scalar, 0, 0, HALF)
-        weave(nc.vector.tensor_copy, w_grouped[1], w_rows[1], 0, P)
+        look_up(nc.vector, 0, 0, HALF)
         minimum(y_early[:], S + HALF, 2 * S)
-        quantize(w_codes[1][:], w_scales[1][:], w_grouped[1][:])
         product(y_joint[:, QUARTER:], 0, 0, HALF)
+        weave(nc.scalar.copy, w_grouped[1], w_rows[1], 0, P)
+
+        scatter(nc.scalar, 0, LATE_SCATTER, S)
+        look_up(nc.scalar, 1, QUARTER, QUARTER + OLD1_SCALAR)
+        look_up(nc.vector, 1, 0, QUARTER)
+        quantize(w_codes[1][:], w_scales[1][:], w_grouped[1][:])
         product(y_lead[:], 1, 0, QUARTER)
         product(y_joint[:, :QUARTER], 1, S - QUARTER, QUARTER)
         product(y_rest[:], 1, QUARTER, HALF)
-
-        scatter(nc.scalar, 0, LATE_SCATTER, S)
-        look_up(nc.vector, 1, 0, QUARTER)
-        look_up(nc.vector, 1, QUARTER, S)
+        look_up(nc.vector, 1, QUARTER + OLD1_SCALAR, S)
         minimum(y_lead[:], 0, QUARTER)
         scatter(nc.scalar, 1, 0, QUARTER)
         minimum(y_joint[:], S - QUARTER, S + HALF)

@@ -68,15 +68,13 @@ def tile_picked_idxput_min_e_kernel(tc, xT, mem, w1, offs, slot, out):
         quantize(w_codes[0][:], w_scales[0][:], w_grouped[0][:])
 
         picked = sb.tile([P, S, PACK], BF16, name="picked", align_bytes=64)
-        planes = [sb.tile([P, 2, QUARTER], BF16, name=f"planes{u}") for u in range(2)]
+        planes = sb.tile([P, PACK, QUARTER], BF16, name="planes")
         for j in range(PACK):
-            u = j // 2
-            nc.scalar.activation(planes[u][:, j % 2, :], x_rows[j][:].indirect(entries(offs_sb, 0, QUARTER)), COPY)
-            if j % 2 == 1:
-                nc.scalar.copy(picked[:, :QUARTER, 2 * u : 2 * u + 2], planes[u][:].rearrange("p j c -> p c j"))
+            nc.scalar.activation(planes[:, j, :], x_rows[j][:].indirect(entries(offs_sb, 0, QUARTER)), COPY)
             pieces = [(QUARTER, S)] if j < PACK - 1 else [(HALF, S), (QUARTER, HALF)]
             for first, last in pieces:
                 nc.vector.tensor_copy(picked[:, first:last, j], x_rows[j][:].indirect(entries(offs_sb, first, last)))
+        weave(nc.scalar.copy, picked, planes, 0, QUARTER)
 
         x_codes = sb.tile([P, S], U32, name="x_codes", align_bytes=64)
         x_scales = sb.tile([P, S], U8, name="x_scales", align_bytes=64)

@@ -19,8 +19,9 @@ PACK = 4
 LIST_ROWS = 16
 HALF = S // 2
 QUARTER = S // 4
-LATE_SCATTER = 352
-OLD1_SCALAR = 128
+GATHER_SCALAR = 192
+PIECE = 64
+LATE_SCATTER = 288
 
 
 def entries(index_tile, first, last):
@@ -48,8 +49,8 @@ def tile_picked_idxput_min_e_kernel(tc, xT, mem, w1, offs, slot, out):
         nc.sync.dma_start(slot_sb[:], slot)
         nc.sync.dma_start(x_rows[2][:], x_by_row[:, 2, :])
         nc.sync.dma_start(x_rows[3][:], x_by_row[:, 3, :])
-        nc.sync.dma_start(store[0][:], mem[0:P, :])
         nc.sync.dma_start(w_rows[1][:], w_by_row[:, :, P:])
+        nc.sync.dma_start(store[0][:], mem[0:P, :])
         nc.sync.dma_start(store[1][:], mem[P : 2 * P, :])
 
         def weave(copy, grouped, rows, first, last):
@@ -68,18 +69,23 @@ def tile_picked_idxput_min_e_kernel(tc, xT, mem, w1, offs, slot, out):
         quantize(w_codes[0][:], w_scales[0][:], w_grouped[0][:])
 
         picked = sb.tile([P, S, PACK], BF16, name="picked", align_bytes=64)
-        planes = sb.tile([P, PACK, QUARTER], BF16, name="planes")
+        planes = sb.tile([P, PACK, GATHER_SCALAR], BF16, name="planes")
+        woven_by_scalar = [(0, PIECE), (PIECE, QUARTER)]
         for j in range(PACK):
-            nc.scalar.activation(planes[:, j, :], x_rows[j][:].indirect(entries(offs_sb, 0, QUARTER)), COPY)
-            pieces = [(QUARTER, S)] if j < PACK - 1 else [(HALF, S), (QUARTER, HALF)]
+            pieces = [(0, GATHER_SCALAR)] if j < PACK - 1 else [(QUARTER, GATHER_SCALAR)] + woven_by_scalar
             for first, last in pieces:
-                nc.vector.tensor_copy(picked[:, first:last, j], x_rows[j][:].indirect(entries(offs_sb, first, last)))
-        weave(nc.scalar.copy, picked, planes, 0, QUARTER)
+                nc.scalar.activation(planes[:, j, first:last], x_rows[j][:].indirect(entries(offs_sb, first, last)), COPY)
+            nc.vector.tensor_copy(picked[:, GATHER_SCALAR:, j], x_rows[j][:].indirect(entries(offs_sb, GATHER_SCALAR, S)))
+        for first, last in woven_by_scalar:
+            weave(nc.scalar.copy, picked, planes, first, last)
+        weave(nc.vector.tensor_copy, picked, planes, QUARTER, GATHER_SCALAR)
 
         x_codes = sb.tile([P, S], U32, name="x_codes", align_bytes=64)
         x_scales = sb.tile([P, S], U8, name="x_scales", align_bytes=64)
-        for cols in (slice(HALF, S), slice(0, HALF)):
-            quantize(x_codes[:, cols], x_scales[:, cols], picked[:, cols, :])
+        quantize(x_codes[:, HALF:], x_scales[:, HALF:], picked[:, HALF:, :])
+        weave(nc.vector.tensor_copy, w_grouped[1], w_rows[1], 0, P)
+        quantize(x_codes[:, :HALF], x_scales[:, :HALF], picked[:, :HALF, :])
+        quantize(w_codes[1][:], w_scales[1][:], w_grouped[1][:])
 
         def product(y, b, first, width):
             cols = slice(first, first + width)
@@ -120,20 +126,17 @@ def tile_picked_idxput_min_e_kernel(tc, xT, mem, w1, offs, slot, out):
         y_rest = psum.tile([P, HALF], F32, name="y_rest")
 
         product(y_early[:], 0, HALF, HALF)
-        look_up(nc.scalar, 0, HALF, S)
-        look_up(nc.vector, 0, 0, HALF)
-        minimum(y_early[:], S + HALF, 2 * S)
-        product(y_joint[:, QUARTER:], 0, 0, HALF)
-        weave(nc.scalar.copy, w_grouped[1], w_rows[1], 0, P)
-
-        scatter(nc.scalar, 0, LATE_SCATTER, S)
-        look_up(nc.scalar, 1, QUARTER, QUARTER + OLD1_SCALAR)
-        look_up(nc.vector, 1, 0, QUARTER)
-        quantize(w_codes[1][:], w_scales[1][:], w_grouped[1][:])
         product(y_lead[:], 1, 0, QUARTER)
+        product(y_joint[:, QUARTER:], 0, 0, HALF)
         product(y_joint[:, :QUARTER], 1, S - QUARTER, QUARTER)
         product(y_rest[:], 1, QUARTER, HALF)
-        look_up(nc.vector, 1, QUARTER + OLD1_SCALAR, S)
+
+        look_up(nc.scalar, 0, HALF, S)
+        look_up(nc.scalar, 0, 0, HALF)
+        minimum(y_early[:], S + HALF, 2 * S)
+        scatter(nc.scalar, 0, LATE_SCATTER, S)
+        look_up(nc.vector, 1, 0, QUARTER)
+        look_up(nc.vector, 1, QUARTER, S)
         minimum(y_lead[:], 0, QUARTER)
         scatter(nc.scalar, 1, 0, QUARTER)
         minimum(y_joint[:], S - QUARTER, S + HALF)

@@ -21,7 +21,7 @@ HALF = S // 2
 QUARTER = S // 4
 GATHER_SCALAR = 192
 PIECE = 64
-LATE_SCATTER = 288
+LATE = 288
 
 
 def entries(index_tile, first, last):
@@ -46,10 +46,10 @@ def tile_picked_idxput_min_e_kernel(tc, xT, mem, w1, offs, slot, out):
         nc.sync.dma_start(x_rows[0][:], x_by_row[:, 0, :])
         nc.sync.dma_start(offs_sb[:], offs)
         nc.sync.dma_start(x_rows[1][:], x_by_row[:, 1, :])
-        nc.sync.dma_start(slot_sb[:], slot)
         nc.sync.dma_start(x_rows[2][:], x_by_row[:, 2, :])
         nc.sync.dma_start(x_rows[3][:], x_by_row[:, 3, :])
         nc.sync.dma_start(w_rows[1][:], w_by_row[:, :, P:])
+        nc.sync.dma_start(slot_sb[:], slot)
         nc.sync.dma_start(store[0][:], mem[0:P, :])
         nc.sync.dma_start(store[1][:], mem[P : 2 * P, :])
 
@@ -83,7 +83,8 @@ def tile_picked_idxput_min_e_kernel(tc, xT, mem, w1, offs, slot, out):
         x_codes = sb.tile([P, S], U32, name="x_codes", align_bytes=64)
         x_scales = sb.tile([P, S], U8, name="x_scales", align_bytes=64)
         quantize(x_codes[:, HALF:], x_scales[:, HALF:], picked[:, HALF:, :])
-        weave(nc.vector.tensor_copy, w_grouped[1], w_rows[1], 0, P)
+        weave(nc.vector.tensor_copy, w_grouped[1], w_rows[1], 0, PIECE)
+        weave(nc.scalar.copy, w_grouped[1], w_rows[1], PIECE, P)
         quantize(x_codes[:, :HALF], x_scales[:, :HALF], picked[:, :HALF, :])
         quantize(w_codes[1][:], w_scales[1][:], w_grouped[1][:])
 
@@ -120,28 +121,33 @@ def tile_picked_idxput_min_e_kernel(tc, xT, mem, w1, offs, slot, out):
         def minimum(y, first, last):
             nc.vector.tensor_tensor(new[:, first:last], y, old[:, first:last], MIN)
 
-        y_early = psum.tile([P, HALF], F32, name="y_early")
+        y_first = psum.tile([P, QUARTER], F32, name="y_first")
+        y_second = psum.tile([P, QUARTER], F32, name="y_second")
         y_lead = psum.tile([P, QUARTER], F32, name="y_lead")
         y_joint = psum.tile([P, QUARTER + HALF], F32, name="y_joint")
         y_rest = psum.tile([P, HALF], F32, name="y_rest")
 
-        product(y_early[:], 0, HALF, HALF)
+        product(y_first[:], 0, S - QUARTER, QUARTER)
+        product(y_second[:], 0, HALF, QUARTER)
         product(y_lead[:], 1, 0, QUARTER)
         product(y_joint[:, QUARTER:], 0, 0, HALF)
         product(y_joint[:, :QUARTER], 1, S - QUARTER, QUARTER)
         product(y_rest[:], 1, QUARTER, HALF)
 
-        look_up(nc.scalar, 0, HALF, S)
-        look_up(nc.scalar, 0, 0, HALF)
-        minimum(y_early[:], S + HALF, 2 * S)
-        scatter(nc.scalar, 0, LATE_SCATTER, S)
+        look_up(nc.scalar, 0, S - QUARTER, S)
+        look_up(nc.scalar, 0, HALF, S - QUARTER)
+        look_up(nc.scalar, 0, PIECE, HALF)
+        look_up(nc.vector, 0, 0, PIECE)
+        minimum(y_first[:], 2 * S - QUARTER, 2 * S)
+        minimum(y_second[:], S + HALF, 2 * S - QUARTER)
+        scatter(nc.scalar, 0, LATE, S)
         look_up(nc.vector, 1, 0, QUARTER)
         look_up(nc.vector, 1, QUARTER, S)
         minimum(y_lead[:], 0, QUARTER)
         scatter(nc.scalar, 1, 0, QUARTER)
         minimum(y_joint[:], S - QUARTER, S + HALF)
         minimum(y_rest[:], QUARTER, S - QUARTER)
-        scatter(nc.vector, 0, 0, LATE_SCATTER)
+        scatter(nc.vector, 0, 0, LATE)
         nc.sync.dma_start(out[0:P, :], store[0][:])
         scatter(nc.scalar, 1, QUARTER, S)
         nc.sync.dma_start(out[P : 2 * P, :], store[1][:])

@@ -19,9 +19,10 @@ PACK = 4
 LIST_ROWS = 16
 HALF = S // 2
 QUARTER = S // 4
-GATHER_SCALAR = 192
+X_VECTOR = 320
 PIECE = 64
-LATE = 288
+EARLY = 224
+W_AT = 64
 
 
 def entries(index_tile, first, last):
@@ -37,117 +38,114 @@ def tile_picked_idxput_min_e_kernel(tc, xT, mem, w1, offs, slot, out):
         offs_sb = sb.tile([P, S // LIST_ROWS], U16, name="offs_sb")
         slot_sb = sb.tile([P, S // LIST_ROWS], U16, name="slot_sb")
         x_rows = [sb.tile([P, T], F32, name=f"x_rows{j}") for j in range(PACK)]
-        w_rows = [sb.tile([P, PACK, P], F32, name=f"w_rows{b}") for b in range(2)]
         store = [sb.tile([P, U], F32, name=f"store{b}") for b in range(2)]
+        table1 = sb.tile([P, U], F32, name="table1")
+        tables = (store[0], table1)
+        old = sb.tile([P, 2 * S], F32, name="old")
+        new = sb.tile([P, 2 * S], F32, name="new")
+        w_first = sb.tile([P, PACK, P], F32, name="w_first")
+        w_rows = (w_first[:], new[:, W_AT : W_AT + PACK * P].rearrange("p (j m) -> p j m", j=PACK))
 
         x_by_row = xT.rearrange("(p j) t -> p j t", j=PACK)
         w_by_row = w1.rearrange("(p j) m -> p j m", j=PACK)
-        nc.sync.dma_start(w_rows[0][:], w_by_row[:, :, :P])
+        nc.sync.dma_start(w_rows[0], w_by_row[:, :, :P])
         nc.sync.dma_start(x_rows[0][:], x_by_row[:, 0, :])
         nc.sync.dma_start(offs_sb[:], offs)
         nc.sync.dma_start(x_rows[1][:], x_by_row[:, 1, :])
         nc.sync.dma_start(x_rows[2][:], x_by_row[:, 2, :])
         nc.sync.dma_start(x_rows[3][:], x_by_row[:, 3, :])
-        nc.sync.dma_start(w_rows[1][:], w_by_row[:, :, P:])
         nc.sync.dma_start(slot_sb[:], slot)
         nc.sync.dma_start(store[0][:], mem[0:P, :])
+        nc.sync.dma_start(w_rows[1], w_by_row[:, :, P:])
+        nc.sync.dma_start(table1[:], mem[P : 2 * P, :])
         nc.sync.dma_start(store[1][:], mem[P : 2 * P, :])
 
-        def weave(copy, grouped, rows, first, last):
-            copy(
-                grouped[:, first:last, :].rearrange("p (c i) j -> p c j i", i=4),
-                rows[:, :, first:last].rearrange("p j (c i) -> p c j i", i=4),
-            )
+        def weave(copy, grouped, rows):
+            copy(grouped.rearrange("p (c i) j -> p c j i", i=4), rows.rearrange("p j (c i) -> p c j i", i=4))
 
         def quantize(codes, scales, grouped):
             nc.vector.quantize_mx(out=codes.bitcast(FP8X4), scales=scales, in_=grouped.rearrange("p c j -> p (c j)"))
 
-        w_grouped = [sb.tile([P, P, PACK], BF16, name=f"w_grouped{b}", align_bytes=64) for b in range(2)]
-        w_codes = [sb.tile([P, P], U32, name=f"w_codes{b}", align_bytes=64) for b in range(2)]
-        w_scales = [sb.tile([P, P], U8, name=f"w_scales{b}", align_bytes=64) for b in range(2)]
-        weave(nc.scalar.copy, w_grouped[0], w_rows[0], 0, P)
-        quantize(w_codes[0][:], w_scales[0][:], w_grouped[0][:])
-
         picked = sb.tile([P, S, PACK], BF16, name="picked", align_bytes=64)
-        planes = sb.tile([P, PACK, GATHER_SCALAR], BF16, name="planes")
-        woven_by_scalar = [(0, PIECE), (PIECE, QUARTER)]
+        planes = sb.tile([P, PACK, S - X_VECTOR], BF16, name="planes")
+        pieces = [(first, first + PIECE) for first in range(X_VECTOR, S, PIECE)]
         for j in range(PACK):
-            pieces = [(0, GATHER_SCALAR)] if j < PACK - 1 else [(QUARTER, GATHER_SCALAR)] + woven_by_scalar
-            for first, last in pieces:
-                nc.scalar.activation(planes[:, j, first:last], x_rows[j][:].indirect(entries(offs_sb, first, last)), COPY)
-            nc.vector.tensor_copy(picked[:, GATHER_SCALAR:, j], x_rows[j][:].indirect(entries(offs_sb, GATHER_SCALAR, S)))
-        for first, last in woven_by_scalar:
-            weave(nc.scalar.copy, picked, planes, first, last)
-        weave(nc.vector.tensor_copy, picked, planes, QUARTER, GATHER_SCALAR)
+            for first, last in [(X_VECTOR, S)] if j < PACK - 1 else pieces:
+                nc.scalar.activation(
+                    planes[:, j, first - X_VECTOR : last - X_VECTOR], x_rows[j][:].indirect(entries(offs_sb, first, last)), COPY
+                )
+            nc.vector.tensor_copy(picked[:, :X_VECTOR, j], x_rows[j][:].indirect(entries(offs_sb, 0, X_VECTOR)))
+        for (first, last), copy in zip(pieces, (nc.vector.tensor_copy, nc.scalar.copy, nc.scalar.copy)):
+            weave(copy, picked[:, first:last, :], planes[:, :, first - X_VECTOR : last - X_VECTOR])
 
         x_codes = sb.tile([P, S], U32, name="x_codes", align_bytes=64)
         x_scales = sb.tile([P, S], U8, name="x_scales", align_bytes=64)
-        quantize(x_codes[:, HALF:], x_scales[:, HALF:], picked[:, HALF:, :])
-        weave(nc.vector.tensor_copy, w_grouped[1], w_rows[1], 0, PIECE)
-        weave(nc.scalar.copy, w_grouped[1], w_rows[1], PIECE, P)
         quantize(x_codes[:, :HALF], x_scales[:, :HALF], picked[:, :HALF, :])
-        quantize(w_codes[1][:], w_scales[1][:], w_grouped[1][:])
+        quantize(x_codes[:, HALF : S - QUARTER], x_scales[:, HALF : S - QUARTER], picked[:, HALF : S - QUARTER, :])
+        quantize(x_codes[:, S - QUARTER :], x_scales[:, S - QUARTER :], picked[:, S - QUARTER :, :])
 
-        def product(y, b, first, width):
-            cols = slice(first, first + width)
+        w_grouped = [sb.tile([P, P, PACK], BF16, name=f"w_grouped{b}", align_bytes=64) for b in range(2)]
+        w_codes = [sb.tile([P, P], U32, name=f"w_codes{b}", align_bytes=64) for b in range(2)]
+        w_scales = [sb.tile([P, P], U8, name=f"w_scales{b}", align_bytes=64) for b in range(2)]
+        weave(nc.scalar.copy, w_grouped[0][:], w_rows[0])
+        quantize(w_codes[0][:], w_scales[0][:], w_grouped[0][:])
+
+        def product(y, b, first, last):
             nc.tensor.matmul_mx(
                 out=y,
                 lhsT=w_codes[b][:].bitcast(FP8X4),
                 lhsT_scale=w_scales[b][:],
-                rhs=x_codes[:, cols].bitcast(FP8X4),
-                rhs_scale=x_scales[:, cols],
+                rhs=x_codes[:, first:last].bitcast(FP8X4),
+                rhs_scale=x_scales[:, first:last],
                 start=True,
                 stop=True,
             )
 
-        old = sb.tile([P, 2 * S], F32, name="old")
-        new = sb.tile([P, 2 * S], F32, name="new")
-        base = (S, 0)
+        def move(engine, target, source):
+            if engine is nc.vector:
+                nc.vector.tensor_copy(target, source)
+            else:
+                nc.scalar.activation(target, source, COPY)
 
         def look_up(engine, b, first, last):
-            window = store[b][:].indirect(entries(slot_sb, first, last))
-            if engine is nc.vector:
-                nc.vector.tensor_copy(old[:, base[b] + first : base[b] + last], window)
-            else:
-                nc.scalar.activation(old[:, base[b] + first : base[b] + last], window, COPY)
+            move(engine, old[:, b * S + first : b * S + last], tables[b][:].indirect(entries(slot_sb, first, last)))
 
         def scatter(engine, b, first, last):
-            window = store[b][:].indirect(entries(slot_sb, first, last))
-            if engine is nc.vector:
-                nc.vector.tensor_copy(window, new[:, base[b] + first : base[b] + last])
-            else:
-                nc.scalar.activation(window, new[:, base[b] + first : base[b] + last], COPY)
+            move(engine, store[b][:].indirect(entries(slot_sb, first, last)), new[:, b * S + first : b * S + last])
 
         def minimum(y, first, last):
             nc.vector.tensor_tensor(new[:, first:last], y, old[:, first:last], MIN)
 
         y_first = psum.tile([P, QUARTER], F32, name="y_first")
         y_second = psum.tile([P, QUARTER], F32, name="y_second")
+        y_joint = psum.tile([P, HALF + QUARTER], F32, name="y_joint")
         y_lead = psum.tile([P, QUARTER], F32, name="y_lead")
-        y_joint = psum.tile([P, QUARTER + HALF], F32, name="y_joint")
         y_rest = psum.tile([P, HALF], F32, name="y_rest")
 
-        product(y_first[:], 0, S - QUARTER, QUARTER)
-        product(y_second[:], 0, HALF, QUARTER)
-        product(y_lead[:], 1, 0, QUARTER)
-        product(y_joint[:, QUARTER:], 0, 0, HALF)
-        product(y_joint[:, :QUARTER], 1, S - QUARTER, QUARTER)
-        product(y_rest[:], 1, QUARTER, HALF)
+        product(y_first[:], 0, 0, QUARTER)
+        product(y_second[:], 0, QUARTER, HALF)
+        product(y_joint[:, :HALF], 0, HALF, S)
+        look_up(nc.scalar, 0, 0, HALF)
+        look_up(nc.scalar, 0, HALF, S)
 
-        look_up(nc.scalar, 0, S - QUARTER, S)
-        look_up(nc.scalar, 0, HALF, S - QUARTER)
-        look_up(nc.scalar, 0, PIECE, HALF)
-        look_up(nc.vector, 0, 0, PIECE)
-        minimum(y_first[:], 2 * S - QUARTER, 2 * S)
-        minimum(y_second[:], S + HALF, 2 * S - QUARTER)
-        scatter(nc.scalar, 0, LATE, S)
+        weave(nc.vector.tensor_copy, w_grouped[1][:, :PIECE, :], w_rows[1][:, :, :PIECE])
+        weave(nc.vector.tensor_copy, w_grouped[1][:, PIECE:, :], w_rows[1][:, :, PIECE:])
+        minimum(y_first[:], 0, QUARTER)
+        minimum(y_second[:], QUARTER, HALF)
+        quantize(w_codes[1][:], w_scales[1][:], w_grouped[1][:])
+        scatter(nc.scalar, 0, 0, EARLY)
+
+        product(y_lead[:], 1, S - QUARTER, S)
+        product(y_joint[:, HALF:], 1, 0, QUARTER)
+        product(y_rest[:], 1, QUARTER, S - QUARTER)
+        look_up(nc.vector, 1, S - QUARTER, S)
         look_up(nc.vector, 1, 0, QUARTER)
-        look_up(nc.vector, 1, QUARTER, S)
-        minimum(y_lead[:], 0, QUARTER)
-        scatter(nc.scalar, 1, 0, QUARTER)
-        minimum(y_joint[:], S - QUARTER, S + HALF)
-        minimum(y_rest[:], QUARTER, S - QUARTER)
-        scatter(nc.vector, 0, 0, LATE)
+        minimum(y_lead[:], 2 * S - QUARTER, 2 * S)
+        scatter(nc.scalar, 1, S - QUARTER, S)
+        look_up(nc.vector, 1, QUARTER, S - QUARTER)
+        minimum(y_joint[:], HALF, S + QUARTER)
+        minimum(y_rest[:], S + QUARTER, 2 * S - QUARTER)
+        scatter(nc.vector, 0, EARLY, S)
         nc.sync.dma_start(out[0:P, :], store[0][:])
-        scatter(nc.scalar, 1, QUARTER, S)
+        scatter(nc.scalar, 1, 0, S - QUARTER)
         nc.sync.dma_start(out[P : 2 * P, :], store[1][:])

@@ -39,8 +39,6 @@ def tile_picked_idxput_min_e_kernel(tc, xT, mem, w1, offs, slot, out):
         slot_sb = sb.tile([P, S // LIST_ROWS], U16, name="slot_sb")
         x_rows = [sb.tile([P, T], F32, name=f"x_rows{j}") for j in range(PACK)]
         store = [sb.tile([P, U], F32, name=f"store{b}") for b in range(2)]
-        table1 = sb.tile([P, U], F32, name="table1")
-        tables = (store[0], table1)
         old = sb.tile([P, 2 * S], F32, name="old")
         new = sb.tile([P, 2 * S], F32, name="new")
         w_first = sb.tile([P, PACK, P], F32, name="w_first")
@@ -57,7 +55,6 @@ def tile_picked_idxput_min_e_kernel(tc, xT, mem, w1, offs, slot, out):
         nc.sync.dma_start(slot_sb[:], slot)
         nc.sync.dma_start(store[0][:], mem[0:P, :])
         nc.sync.dma_start(w_rows[1], w_by_row[:, :, P:])
-        nc.sync.dma_start(table1[:], mem[P : 2 * P, :])
         nc.sync.dma_start(store[1][:], mem[P : 2 * P, :])
 
         def weave(copy, grouped, rows):
@@ -68,21 +65,26 @@ def tile_picked_idxput_min_e_kernel(tc, xT, mem, w1, offs, slot, out):
 
         picked = sb.tile([P, S, PACK], BF16, name="picked", align_bytes=64)
         planes = sb.tile([P, PACK, S - X_VECTOR], BF16, name="planes")
-        pieces = [(first, first + PIECE) for first in range(X_VECTOR, S, PIECE)]
+        middle = (X_VECTOR + S) // 2
         for j in range(PACK):
-            for first, last in [(X_VECTOR, S)] if j < PACK - 1 else pieces:
+            last_row = j == PACK - 1
+            by_scalar = [(X_VECTOR, middle), (middle, S)] if last_row else [(X_VECTOR, S)]
+            by_vector = [(0, QUARTER), (QUARTER, X_VECTOR)] if last_row else [(0, X_VECTOR)]
+            for first, last in by_scalar:
                 nc.scalar.activation(
                     planes[:, j, first - X_VECTOR : last - X_VECTOR], x_rows[j][:].indirect(entries(offs_sb, first, last)), COPY
                 )
-            nc.vector.tensor_copy(picked[:, :X_VECTOR, j], x_rows[j][:].indirect(entries(offs_sb, 0, X_VECTOR)))
-        for (first, last), copy in zip(pieces, (nc.vector.tensor_copy, nc.scalar.copy, nc.scalar.copy)):
-            weave(copy, picked[:, first:last, :], planes[:, :, first - X_VECTOR : last - X_VECTOR])
+            for first, last in by_vector:
+                nc.vector.tensor_copy(picked[:, first:last, j], x_rows[j][:].indirect(entries(offs_sb, first, last)))
+            if j % 2 == 1:
+                for first, last in by_scalar:
+                    pair = planes[:, j - 1 : j + 1, first - X_VECTOR : last - X_VECTOR]
+                    nc.scalar.copy(picked[:, first:last, j - 1 : j + 1], pair.rearrange("p j c -> p c j"))
 
         x_codes = sb.tile([P, S], U32, name="x_codes", align_bytes=64)
         x_scales = sb.tile([P, S], U8, name="x_scales", align_bytes=64)
-        quantize(x_codes[:, :HALF], x_scales[:, :HALF], picked[:, :HALF, :])
-        quantize(x_codes[:, HALF : S - QUARTER], x_scales[:, HALF : S - QUARTER], picked[:, HALF : S - QUARTER, :])
-        quantize(x_codes[:, S - QUARTER :], x_scales[:, S - QUARTER :], picked[:, S - QUARTER :, :])
+        for first, last in ((0, QUARTER), (QUARTER, HALF), (HALF, S)):
+            quantize(x_codes[:, first:last], x_scales[:, first:last], picked[:, first:last, :])
 
         w_grouped = [sb.tile([P, P, PACK], BF16, name=f"w_grouped{b}", align_bytes=64) for b in range(2)]
         w_codes = [sb.tile([P, P], U32, name=f"w_codes{b}", align_bytes=64) for b in range(2)]
@@ -108,7 +110,7 @@ def tile_picked_idxput_min_e_kernel(tc, xT, mem, w1, offs, slot, out):
                 nc.scalar.activation(target, source, COPY)
 
         def look_up(engine, b, first, last):
-            move(engine, old[:, b * S + first : b * S + last], tables[b][:].indirect(entries(slot_sb, first, last)))
+            move(engine, old[:, b * S + first : b * S + last], store[b][:].indirect(entries(slot_sb, first, last)))
 
         def scatter(engine, b, first, last):
             move(engine, store[b][:].indirect(entries(slot_sb, first, last)), new[:, b * S + first : b * S + last])
@@ -140,9 +142,9 @@ def tile_picked_idxput_min_e_kernel(tc, xT, mem, w1, offs, slot, out):
         product(y_rest[:], 1, QUARTER, S - QUARTER)
         look_up(nc.vector, 1, S - QUARTER, S)
         look_up(nc.vector, 1, 0, QUARTER)
+        look_up(nc.vector, 1, QUARTER, S - QUARTER)
         minimum(y_lead[:], 2 * S - QUARTER, 2 * S)
         scatter(nc.scalar, 1, S - QUARTER, S)
-        look_up(nc.vector, 1, QUARTER, S - QUARTER)
         minimum(y_joint[:], HALF, S + QUARTER)
         minimum(y_rest[:], S + QUARTER, 2 * S - QUARTER)
         scatter(nc.vector, 0, EARLY, S)

@@ -19,7 +19,7 @@ PACK = 4
 LIST_ROWS = 16
 HALF = S // 2
 QUARTER = S // 4
-X_VECTOR = 320
+X_VECTOR = 288
 PIECE = 64
 EARLY = 224
 W_AT = 64
@@ -64,22 +64,11 @@ def tile_picked_idxput_min_e_kernel(tc, xT, mem, w1, offs, slot, out):
             nc.vector.quantize_mx(out=codes.bitcast(FP8X4), scales=scales, in_=grouped.rearrange("p c j -> p (c j)"))
 
         picked = sb.tile([P, S, PACK], BF16, name="picked", align_bytes=64)
-        planes = sb.tile([P, PACK, S - X_VECTOR], BF16, name="planes")
-        middle = (X_VECTOR + S) // 2
         for j in range(PACK):
-            last_row = j == PACK - 1
-            by_scalar = [(X_VECTOR, middle), (middle, S)] if last_row else [(X_VECTOR, S)]
-            by_vector = [(0, QUARTER), (QUARTER, X_VECTOR)] if last_row else [(0, X_VECTOR)]
-            for first, last in by_scalar:
-                nc.scalar.activation(
-                    planes[:, j, first - X_VECTOR : last - X_VECTOR], x_rows[j][:].indirect(entries(offs_sb, first, last)), COPY
-                )
+            by_vector = [(0, QUARTER), (QUARTER, X_VECTOR)] if j == PACK - 1 else [(0, X_VECTOR)]
+            nc.scalar.activation(picked[:, X_VECTOR:, j], x_rows[j][:].indirect(entries(offs_sb, X_VECTOR, S)), COPY)
             for first, last in by_vector:
                 nc.vector.tensor_copy(picked[:, first:last, j], x_rows[j][:].indirect(entries(offs_sb, first, last)))
-            if j % 2 == 1:
-                for first, last in by_scalar:
-                    pair = planes[:, j - 1 : j + 1, first - X_VECTOR : last - X_VECTOR]
-                    nc.scalar.copy(picked[:, first:last, j - 1 : j + 1], pair.rearrange("p j c -> p c j"))
 
         x_codes = sb.tile([P, S], U32, name="x_codes", align_bytes=64)
         x_scales = sb.tile([P, S], U8, name="x_scales", align_bytes=64)

from contextlib import ExitStack

import concourse.mybir as mybir

K, T, S, N, U = 512, 1024, 512, 256, 1024
FLOPS = 2 * K * S * N

F32 = mybir.dt.float32
BF16 = mybir.dt.bfloat16
U32 = mybir.dt.uint32
U16 = mybir.dt.uint16
U8 = mybir.dt.uint8
FP8X4 = mybir.dt.float8_e4m3fn_x4
COPY = mybir.ActivationFunctionType.Copy
MIN = mybir.AluOpType.min

P = 128
PACK = 4
LIST_ROWS = 16
HALF = S // 2
QUARTER = S // 4
X_VECTOR = 288
PIECE = 64
EARLY = 224
W_AT = 64


def entries(index_tile, first, last):
    return index_tile[:, first // LIST_ROWS : last // LIST_ROWS]


def tile_picked_idxput_min_e_kernel(tc, xT, mem, w1, offs, slot, out):
    nc = tc.nc
    with ExitStack() as ctx:
        sb = ctx.enter_context(tc.tile_pool(name="sb", bufs=1))
        psum = ctx.enter_context(tc.psum_pool(name="psum", bufs=1))

        offs_sb = sb.tile([P, S // LIST_ROWS], U16, name="offs_sb")
        slot_sb = sb.tile([P, S // LIST_ROWS], U16, name="slot_sb")
        x_rows = [sb.tile([P, T], F32, name=f"x_rows{j}") for j in range(PACK)]
        store = [sb.tile([P, U], F32, name=f"store{b}") for b in range(2)]
        old = sb.tile([P, 2 * S], F32, name="old")
        new = sb.tile([P, 2 * S], F32, name="new")
        w_first = sb.tile([P, PACK, P], F32, name="w_first")
        w_rows = (w_first[:], new[:, W_AT : W_AT + PACK * P].rearrange("p (j m) -> p j m", j=PACK))

        x_by_row = xT.rearrange("(p j) t -> p j t", j=PACK)
        w_by_row = w1.rearrange("(p j) m -> p j m", j=PACK)
        nc.sync.dma_start(w_rows[0], w_by_row[:, :, :P])
        nc.sync.dma_start(x_rows[0][:], x_by_row[:, 0, :])
        nc.sync.dma_start(offs_sb[:], offs)
        nc.sync.dma_start(x_rows[1][:], x_by_row[:, 1, :])
        nc.sync.dma_start(x_rows[2][:], x_by_row[:, 2, :])
        nc.sync.dma_start(x_rows[3][:], x_by_row[:, 3, :])
        nc.sync.dma_start(slot_sb[:], slot)
        nc.sync.dma_start(store[0][:], mem[0:P, :])
        nc.sync.dma_start(w_rows[1], w_by_row[:, :, P:])
        nc.sync.dma_start(store[1][:], mem[P : 2 * P, :])

        def weave(copy, grouped, rows):
            copy(grouped.rearrange("p (c i) j -> p c j i", i=4), rows.rearrange("p j (c i) -> p c j i", i=4))

        def quantize(codes, scales, grouped):
            nc.vector.quantize_mx(out=codes.bitcast(FP8X4), scales=scales, in_=grouped.rearrange("p c j -> p (c j)"))

        picked = sb.tile([P, S, PACK], BF16, name="picked", align_bytes=64)
        for j in range(PACK):
            by_vector = [(0, QUARTER), (QUARTER, X_VECTOR)] if j == PACK - 1 else [(0, X_VECTOR)]
            nc.scalar.activation(picked[:, X_VECTOR:, j], x_rows[j][:].indirect(entries(offs_sb, X_VECTOR, S)), COPY)
            for first, last in by_vector:
                nc.vector.tensor_copy(picked[:, first:last, j], x_rows[j][:].indirect(entries(offs_sb, first, last)))

        x_codes = sb.tile([P, S], U32, name="x_codes", align_bytes=64)
        x_scales = sb.tile([P, S], U8, name="x_scales", align_bytes=64)
        for first, last in ((0, QUARTER), (QUARTER, HALF), (HALF, S)):
            quantize(x_codes[:, first:last], x_scales[:, first:last], picked[:, first:last, :])

        w_grouped = [sb.tile([P, P, PACK], BF16, name=f"w_grouped{b}", align_bytes=64) for b in range(2)]
        w_codes = [sb.tile([P, P], U32, name=f"w_codes{b}", align_bytes=64) for b in range(2)]
        w_scales = [sb.tile([P, P], U8, name=f"w_scales{b}", align_bytes=64) for b in range(2)]
        weave(nc.scalar.copy, w_grouped[0][:], w_rows[0])
        quantize(w_codes[0][:], w_scales[0][:], w_grouped[0][:])

        def product(y, b, first, last):
            nc.tensor.matmul_mx(
                out=y,
                lhsT=w_codes[b][:].bitcast(FP8X4),
                lhsT_scale=w_scales[b][:],
                rhs=x_codes[:, first:last].bitcast(FP8X4),
                rhs_scale=x_scales[:, first:last],
                start=True,
                stop=True,
            )

        def move(engine, target, source):
            if engine is nc.vector:
                nc.vector.tensor_copy(target, source)
            else:
                nc.scalar.activation(target, source, COPY)

        def look_up(engine, b, first, last):
            move(engine, old[:, b * S + first : b * S + last], store[b][:].indirect(entries(slot_sb, first, last)))

        def scatter(engine, b, first, last):
            move(engine, store[b][:].indirect(entries(slot_sb, first, last)), new[:, b * S + first : b * S + last])

        def minimum(y, first, last):
            nc.vector.tensor_tensor(new[:, first:last], y, old[:, first:last], MIN)

        y_first = psum.tile([P, QUARTER], F32, name="y_first")
        y_second = psum.tile([P, QUARTER], F32, name="y_second")
        y_joint = psum.tile([P, HALF + QUARTER], F32, name="y_joint")
        y_lead = psum.tile([P, QUARTER], F32, name="y_lead")
        y_rest = psum.tile([P, HALF], F32, name="y_rest")

        product(y_first[:], 0, 0, QUARTER)
        product(y_second[:], 0, QUARTER, HALF)
        product(y_joint[:, :HALF], 0, HALF, S)
        look_up(nc.scalar, 0, 0, HALF)
        look_up(nc.scalar, 0, HALF, S)

        weave(nc.vector.tensor_copy, w_grouped[1][:, :PIECE, :], w_rows[1][:, :, :PIECE])
        weave(nc.vector.tensor_copy, w_grouped[1][:, PIECE:, :], w_rows[1][:, :, PIECE:])
        minimum(y_first[:], 0, QUARTER)
        minimum(y_second[:], QUARTER, HALF)
        quantize(w_codes[1][:], w_scales[1][:], w_grouped[1][:])
        scatter(nc.scalar, 0, 0, EARLY)

        product(y_lead[:], 1, S - QUARTER, S)
        product(y_joint[:, HALF:], 1, 0, QUARTER)
        product(y_rest[:], 1, QUARTER, S - QUARTER)
        look_up(nc.vector, 1, S - QUARTER, S)
        look_up(nc.vector, 1, 0, QUARTER)
        look_up(nc.vector, 1, QUARTER, S - QUARTER)
        minimum(y_lead[:], 2 * S - QUARTER, 2 * S)
        scatter(nc.scalar, 1, S - QUARTER, S)
        minimum(y_joint[:], HALF, S + QUARTER)
        minimum(y_rest[:], S + QUARTER, 2 * S - QUARTER)
        scatter(nc.vector, 0, EARLY, S)
        nc.sync.dma_start(out[0:P, :], store[0][:])
        scatter(nc.scalar, 1, 0, S - QUARTER)
        nc.sync.dma_start(out[P : 2 * P, :], store[1][:])
